import numpy as np
import ml_dtypes


def mxq(x, axis, fmt="e4m3"):
    dtype, down = {"e4m3": (ml_dtypes.float8_e4m3fn, 7), "e5m2": (ml_dtypes.float8_e5m2, 14)}[fmt]
    v = np.moveaxis(np.asarray(x, np.float32).astype(ml_dtypes.bfloat16).astype(np.float64), axis, -1)
    blocks = v.reshape(v.shape[:-1] + (-1, 32))
    amax = np.abs(blocks).max(-1, keepdims=True)
    byte = np.maximum(np.where(amax > 0, np.frexp(amax)[1] - 1 + 127, 0) - down, 1)
    scale = np.exp2(byte - 127.0)
    codes = (blocks / scale).astype(np.float32).astype(dtype).astype(np.float64)
    return np.moveaxis((codes * scale).reshape(v.shape), -1, axis)


WIDE = False


def mx_kscale(k, group=512):
    if not WIDE:
        return np.ones(k)
    levels = np.array([18, -18])
    if group != 512:
        return np.exp2(np.random.permutation(np.resize(levels, k // group))).repeat(group)
    if k % 512:
        return np.exp2(np.random.permutation(np.resize(levels, k // 32))).repeat(32)
    a = np.empty((k // 512, 16))
    for p in range(k // 512):
        a[p, :8] = np.random.permutation(np.resize(levels, 8))
        for g in range(8):
            far = levels[np.abs(levels - a[p, g]) >= 10]
            a[p, g + 8] = far[np.random.randint(len(far))]
    return np.exp2(a.ravel()).repeat(32)


def f64(x):
    return np.asarray(x).astype(np.float64)


G, D, M, N = 2, 256, 256, 512


def setup_inputs():
    n = np.random.standard_normal
    s_d = mx_kscale(D, 0)
    return {
        "dy": (n((G, D, N)) * s_d[:, None]).astype(np.float32),
        "w": (n((G, D, M)) / np.sqrt(D) / s_d[:, None]).astype(np.float32),
        "mk": (np.random.uniform(size=(G, M, N)) < 0.5).astype(np.float32),
        "gs": (n((G, M, N))).astype(np.float32),
    }


def reference(dy, w, mk, gs):
    wq = mxq(f64(w), 1, "e5m2")
    dyq = mxq(f64(dy), 1, "e5m2")
    z = wq.transpose(0, 2, 1) @ dyq
    y = z * f64(mk) + f64(gs)
    return y

@@ -1,0 +1,98 @@
+from contextlib import ExitStack
+
+import concourse.mybir as mybir
+
+G, D, M, N = 2, 256, 256, 512
+FLOPS = 2 * G * D * M * N
+
+F32 = mybir.dt.float32
+BF16 = mybir.dt.bfloat16
+U32 = mybir.dt.uint32
+U8 = mybir.dt.uint8
+E5M2X4 = mybir.dt.float8_e5m2_x4
+MULT = mybir.AluOpType.mult
+ADD = mybir.AluOpType.add
+
+P = 128
+PACK = 4
+ROWS = D // PACK
+HALVES = M // P
+DVE_COLS = 336
+
+
+def tile_rows_gback_relu_kernel(tc, dy, w, mk, gs, out):
+    nc = tc.nc
+    dy_rows = dy.rearrange("g (p j) n -> (g p) j n", j=PACK)
+    w_rows = w.rearrange("g (p j) m -> (g p) j m", j=PACK)
+    mk_rows = mk.rearrange("g (p h) n -> g p h n", h=HALVES)
+    gs_rows = gs.rearrange("g (p h) n -> g p h n", h=HALVES)
+    out_rows = out.rearrange("g (p h) n -> g p h n", h=HALVES)
+
+    with ExitStack() as ctx:
+        sb = ctx.enter_context(tc.tile_pool(name="sb", bufs=1))
+        psum = ctx.enter_context(tc.psum_pool(name="psum", bufs=1))
+        ctx.enter_context(tc.manual_schedule())
+
+        dy_raw = [sb.tile([P, 2, N], F32, name="dy_raw%d" % u, align_bytes=64) for u in range(2)]
+        w_raw = sb.tile([P, PACK, M], F32, align_bytes=64)
+        mk_sb = [sb.tile([P, HALVES, N], F32, name="mk%d" % g, align_bytes=64) for g in range(G)]
+        gs_sb = [sb.tile([P, HALVES, N], F32, name="gs%d" % g, align_bytes=64) for g in range(G)]
+        masked = [sb.tile([P, HALVES, N], F32, name="masked%d" % g, align_bytes=64) for g in range(G)]
+        res = [sb.tile([P, HALVES, N], F32, name="res%d" % g, align_bytes=64) for g in range(G)]
+        dy_bf = sb.tile([P, N, PACK], BF16, align_bytes=64)
+        dy_codes = sb.tile([P, N], U32, align_bytes=64)
+        dy_scales = sb.tile([P, N], U8, align_bytes=64)
+        w_bf = [sb.tile([P, P, PACK], BF16, name="w_bf%d" % h, align_bytes=64) for h in range(HALVES)]
+        w_codes = [sb.tile([P, P], U32, name="w_codes%d" % h, align_bytes=64) for h in range(HALVES)]
+        w_scales = [sb.tile([P, P], U8, name="w_scales%d" % h, align_bytes=64) for h in range(HALVES)]
+        z = [[psum.tile([P, N], F32, name="z%d%d" % (g, h)) for h in range(HALVES)] for g in range(G)]
+
+        for u in range(2):
+            nc.sync.dma_start(out=dy_raw[u][:], in_=dy_rows[:, 2 * u : 2 * u + 2, :])
+        nc.sync.dma_start(out=w_raw[:], in_=w_rows)
+        nc.sync.dma_start(out=mk_sb[0][:], in_=mk_rows[0])
+        nc.sync.dma_start(out=gs_sb[0][:], in_=gs_rows[0])
+        nc.sync.dma_start(out=mk_sb[1][:], in_=mk_rows[1])
+        for h in range(HALVES):
+            nc.sync.dma_start(out=gs_sb[1][:, h, :], in_=gs_rows[1][:, h, :])
+
+        for u in range(2):
+            src = dy_raw[u][:].rearrange("p j n -> p n j")
+            nc.vector.tensor_copy(out=dy_bf[:, :DVE_COLS, 2 * u : 2 * u + 2], in_=src[:, :DVE_COLS, :])
+            nc.scalar.copy(out=dy_bf[:, DVE_COLS:, 2 * u : 2 * u + 2], in_=src[:, DVE_COLS:, :])
+        nc.vector.quantize_mx(
+            out=dy_codes[:].bitcast(E5M2X4),
+            scales=dy_scales[:],
+            in_=dy_bf[:].rearrange("p n j -> p (n j)"),
+        )
+
+        w_src = w_raw[:].rearrange("p j (s h) -> p h s j", h=HALVES)
+        nc.vector.tensor_copy(out=w_bf[0][:], in_=w_src[:, 0])
+        nc.scalar.copy(out=w_bf[1][:], in_=w_src[:, 1])
+        for h in range(HALVES):
+            nc.vector.quantize_mx(
+                out=w_codes[h][:].bitcast(E5M2X4),
+                scales=w_scales[h][:],
+                in_=w_bf[h][:].rearrange("p s j -> p (s j)"),
+            )
+            for g in range(G):
+                rows = slice(g * ROWS, (g + 1) * ROWS)
+                nc.tensor.matmul_mx(
+                    out=z[g][h][:],
+                    lhsT=w_codes[h][rows, :].bitcast(E5M2X4),
+                    lhsT_scale=w_scales[h][rows, :],
+                    rhs=dy_codes[rows, :].bitcast(E5M2X4),
+                    rhs_scale=dy_scales[rows, :],
+                    start=True,
+                    stop=True,
+                )
+
+        for g in range(G):
+            for h in range(HALVES):
+                nc.vector.tensor_tensor(out=masked[g][:, h, :], in0=z[g][h][:], in1=mk_sb[g][:, h, :], op=MULT)
+            for h in range(HALVES):
+                nc.vector.tensor_tensor(out=res[g][:, h, :], in0=masked[g][:, h, :], in1=gs_sb[g][:, h, :], op=ADD)
+                if g == G - 1:
+                    nc.sync.dma_start(out=out_rows[g][:, h, :], in_=res[g][:, h, :])
+            if g < G - 1:
+                nc.sync.dma_start(out=out_rows[g], in_=res[g][:])

@@ -17,16 +17,18 @@ P = 128
 PACK = 4
 ROWS = D // PACK
 HALVES = M // P
-DVE_COLS = 336
+DY_VECTOR_COLS = 336
+W0_VECTOR_COLS = 64
+W1_VECTOR_COLS = 64
 
 
 def tile_rows_gback_relu_kernel(tc, dy, w, mk, gs, out):
     nc = tc.nc
     dy_rows = dy.rearrange("g (p j) n -> (g p) j n", j=PACK)
     w_rows = w.rearrange("g (p j) m -> (g p) j m", j=PACK)
-    mk_rows = mk.rearrange("g (p h) n -> g p h n", h=HALVES)
-    gs_rows = gs.rearrange("g (p h) n -> g p h n", h=HALVES)
-    out_rows = out.rearrange("g (p h) n -> g p h n", h=HALVES)
+    mk_rows = mk.rearrange("g (h p) n -> h p g n", h=HALVES)
+    gs_rows = gs.rearrange("g (h p) n -> h p g n", h=HALVES)
+    out_rows = out.rearrange("g (h p) n -> h p g n", h=HALVES)
 
     with ExitStack() as ctx:
         sb = ctx.enter_context(tc.tile_pool(name="sb", bufs=1))
@@ -35,40 +37,54 @@ def tile_rows_gback_relu_kernel(tc, dy, w, mk, gs, out):
 
         dy_raw = [sb.tile([P, 2, N], F32, name="dy_raw%d" % u, align_bytes=64) for u in range(2)]
         w_raw = sb.tile([P, PACK, M], F32, align_bytes=64)
-        mk_sb = [sb.tile([P, HALVES, N], F32, name="mk%d" % g, align_bytes=64) for g in range(G)]
-        gs_sb = [sb.tile([P, HALVES, N], F32, name="gs%d" % g, align_bytes=64) for g in range(G)]
-        masked = [sb.tile([P, HALVES, N], F32, name="masked%d" % g, align_bytes=64) for g in range(G)]
-        res = [sb.tile([P, HALVES, N], F32, name="res%d" % g, align_bytes=64) for g in range(G)]
+        mk_sb = [sb.tile([P, G, N], F32, name="mk%d" % h, align_bytes=64) for h in range(HALVES)]
+        gs_sb = [sb.tile([P, G, N], F32, name="gs%d" % h, align_bytes=64) for h in range(HALVES)]
+        masked = [sb.tile([P, G, N], F32, name="masked%d" % h, align_bytes=64) for h in range(HALVES)]
+        res = [sb.tile([P, G, N], F32, name="res%d" % h, align_bytes=64) for h in range(HALVES)]
         dy_bf = sb.tile([P, N, PACK], BF16, align_bytes=64)
         dy_codes = sb.tile([P, N], U32, align_bytes=64)
         dy_scales = sb.tile([P, N], U8, align_bytes=64)
         w_bf = [sb.tile([P, P, PACK], BF16, name="w_bf%d" % h, align_bytes=64) for h in range(HALVES)]
         w_codes = [sb.tile([P, P], U32, name="w_codes%d" % h, align_bytes=64) for h in range(HALVES)]
         w_scales = [sb.tile([P, P], U8, name="w_scales%d" % h, align_bytes=64) for h in range(HALVES)]
-        z = [[psum.tile([P, N], F32, name="z%d%d" % (g, h)) for h in range(HALVES)] for g in range(G)]
+        z = [[psum.tile([P, N], F32, name="z%d%d" % (h, g)) for g in range(G)] for h in range(HALVES)]
+
+        def load(dst, src):
+            nc.sync.dma_start(out=dst, in_=src)
+
+        def mask(h, g):
+            nc.vector.tensor_tensor(out=masked[h][:, g, :], in0=z[h][g][:], in1=mk_sb[h][:, g, :], op=MULT)
+
+        def add(h, g, eng, lo=0, hi=N):
+            eng.tensor_tensor(out=res[h][:, g, lo:hi], in0=masked[h][:, g, lo:hi], in1=gs_sb[h][:, g, lo:hi], op=ADD)
+
+        def store(h, g, lo=0, hi=N):
+            nc.sync.dma_start(out=out_rows[h][:, g, lo:hi], in_=res[h][:, g, lo:hi])
 
         for u in range(2):
-            nc.sync.dma_start(out=dy_raw[u][:], in_=dy_rows[:, 2 * u : 2 * u + 2, :])
-        nc.sync.dma_start(out=w_raw[:], in_=w_rows)
-        nc.sync.dma_start(out=mk_sb[0][:], in_=mk_rows[0])
-        nc.sync.dma_start(out=gs_sb[0][:], in_=gs_rows[0])
-        nc.sync.dma_start(out=mk_sb[1][:], in_=mk_rows[1])
-        for h in range(HALVES):
-            nc.sync.dma_start(out=gs_sb[1][:, h, :], in_=gs_rows[1][:, h, :])
+            load(dy_raw[u][:], dy_rows[:, 2 * u : 2 * u + 2, :])
+        load(w_raw[:], w_rows)
+        load(mk_sb[0][:], mk_rows[0])
+        load(gs_sb[0][:, 0, :], gs_rows[0][:, 0, :])
+        load(mk_sb[1][:], mk_rows[1])
+        load(gs_sb[0][:, 1, :], gs_rows[0][:, 1, :])
+        load(gs_sb[1][:, 0, :], gs_rows[1][:, 0, :])
+        load(gs_sb[1][:, 1, :], gs_rows[1][:, 1, :])
 
         for u in range(2):
             src = dy_raw[u][:].rearrange("p j n -> p n j")
-            nc.vector.tensor_copy(out=dy_bf[:, :DVE_COLS, 2 * u : 2 * u + 2], in_=src[:, :DVE_COLS, :])
-            nc.scalar.copy(out=dy_bf[:, DVE_COLS:, 2 * u : 2 * u + 2], in_=src[:, DVE_COLS:, :])
+            nc.vector.tensor_copy(out=dy_bf[:, :DY_VECTOR_COLS, 2 * u : 2 * u + 2], in_=src[:, :DY_VECTOR_COLS, :])
+            nc.scalar.copy(out=dy_bf[:, DY_VECTOR_COLS:, 2 * u : 2 * u + 2], in_=src[:, DY_VECTOR_COLS:, :])
         nc.vector.quantize_mx(
             out=dy_codes[:].bitcast(E5M2X4),
             scales=dy_scales[:],
             in_=dy_bf[:].rearrange("p n j -> p (n j)"),
         )
 
-        w_src = w_raw[:].rearrange("p j (s h) -> p h s j", h=HALVES)
-        nc.vector.tensor_copy(out=w_bf[0][:], in_=w_src[:, 0])
-        nc.scalar.copy(out=w_bf[1][:], in_=w_src[:, 1])
+        w_src = w_raw[:].rearrange("p j (h s) -> p h s j", h=HALVES)
+        for h, cols in enumerate((W0_VECTOR_COLS, W1_VECTOR_COLS)):
+            nc.vector.tensor_copy(out=w_bf[h][:, :cols, :], in_=w_src[:, h, :cols, :])
+            nc.scalar.copy(out=w_bf[h][:, cols:, :], in_=w_src[:, h, cols:, :])
         for h in range(HALVES):
             nc.vector.quantize_mx(
                 out=w_codes[h][:].bitcast(E5M2X4),
@@ -78,7 +94,7 @@ def tile_rows_gback_relu_kernel(tc, dy, w, mk, gs, out):
             for g in range(G):
                 rows = slice(g * ROWS, (g + 1) * ROWS)
                 nc.tensor.matmul_mx(
-                    out=z[g][h][:],
+                    out=z[h][g][:],
                     lhsT=w_codes[h][rows, :].bitcast(E5M2X4),
                     lhsT_scale=w_scales[h][rows, :],
                     rhs=dy_codes[rows, :].bitcast(E5M2X4),
@@ -87,12 +103,15 @@ def tile_rows_gback_relu_kernel(tc, dy, w, mk, gs, out):
                     stop=True,
                 )
 
-        for g in range(G):
-            for h in range(HALVES):
-                nc.vector.tensor_tensor(out=masked[g][:, h, :], in0=z[g][h][:], in1=mk_sb[g][:, h, :], op=MULT)
-            for h in range(HALVES):
-                nc.vector.tensor_tensor(out=res[g][:, h, :], in0=masked[g][:, h, :], in1=gs_sb[g][:, h, :], op=ADD)
-                if g == G - 1:
-                    nc.sync.dma_start(out=out_rows[g][:, h, :], in_=res[g][:, h, :])
-            if g < G - 1:
-                nc.sync.dma_start(out=out_rows[g], in_=res[g][:])
+        mask(0, 0)
+        add(0, 0, nc.gpsimd)
+        store(0, 0)
+        mask(0, 1)
+        mask(1, 0)
+        mask(1, 1)
+        add(0, 1, nc.vector)
+        store(0, 1)
+        add(1, 0, nc.vector)
+        store(1, 0)
+        add(1, 1, nc.vector)
+        store(1, 1)

@@ -17,9 +17,10 @@ P = 128
 PACK = 4
 ROWS = D // PACK
 HALVES = M // P
-DY_VECTOR_COLS = 336
-W0_VECTOR_COLS = 64
-W1_VECTOR_COLS = 64
+DY_LOAD = N // 2
+QUANT = 128
+DY_VECTOR_COLS = 168
+RUN = 4
 
 
 def tile_rows_gback_relu_kernel(tc, dy, w, mk, gs, out):
@@ -35,8 +36,8 @@ def tile_rows_gback_relu_kernel(tc, dy, w, mk, gs, out):
         psum = ctx.enter_context(tc.psum_pool(name="psum", bufs=1))
         ctx.enter_context(tc.manual_schedule())
 
-        dy_raw = [sb.tile([P, 2, N], F32, name="dy_raw%d" % u, align_bytes=64) for u in range(2)]
-        w_raw = sb.tile([P, PACK, M], F32, align_bytes=64)
+        dy_raw = [sb.tile([P, PACK, DY_LOAD], F32, name="dy_raw%d" % u, align_bytes=64) for u in range(2)]
+        w_raw = [sb.tile([P, PACK, P], F32, name="w_raw%d" % h, align_bytes=64) for h in range(HALVES)]
         mk_sb = [sb.tile([P, G, N], F32, name="mk%d" % h, align_bytes=64) for h in range(HALVES)]
         gs_sb = [sb.tile([P, G, N], F32, name="gs%d" % h, align_bytes=64) for h in range(HALVES)]
         masked = [sb.tile([P, G, N], F32, name="masked%d" % h, align_bytes=64) for h in range(HALVES)]
@@ -52,45 +53,29 @@ def tile_rows_gback_relu_kernel(tc, dy, w, mk, gs, out):
         def load(dst, src):
             nc.sync.dma_start(out=dst, in_=src)
 
-        def mask(h, g):
-            nc.vector.tensor_tensor(out=masked[h][:, g, :], in0=z[h][g][:], in1=mk_sb[h][:, g, :], op=MULT)
+        def interleave(copy, dst, src):
+            copy(out=dst.rearrange("p (c i) j -> p c j i", i=RUN), in_=src.rearrange("p j (c i) -> p c j i", i=RUN))
 
-        def add(h, g, eng, lo=0, hi=N):
-            eng.tensor_tensor(out=res[h][:, g, lo:hi], in0=masked[h][:, g, lo:hi], in1=gs_sb[h][:, g, lo:hi], op=ADD)
+        def quantize(codes, scales, values):
+            nc.vector.quantize_mx(out=codes.bitcast(E5M2X4), scales=scales, in_=values.rearrange("p c j -> p (c j)"))
 
-        def store(h, g, lo=0, hi=N):
-            nc.sync.dma_start(out=out_rows[h][:, g, lo:hi], in_=res[h][:, g, lo:hi])
+        def prepare_dy(u):
+            base = u * DY_LOAD
+            for copy, lo, hi in (
+                (nc.vector.tensor_copy, 0, QUANT),
+                (nc.vector.tensor_copy, QUANT, DY_VECTOR_COLS),
+                (nc.scalar.copy, DY_VECTOR_COLS, DY_LOAD),
+            ):
+                interleave(copy, dy_bf[:, base + lo : base + hi, :], dy_raw[u][:, :, lo:hi])
+            for lo in range(base, base + DY_LOAD, QUANT):
+                cols = slice(lo, lo + QUANT)
+                quantize(dy_codes[:, cols], dy_scales[:, cols], dy_bf[:, cols, :])
 
-        for u in range(2):
-            load(dy_raw[u][:], dy_rows[:, 2 * u : 2 * u + 2, :])
-        load(w_raw[:], w_rows)
-        load(mk_sb[0][:], mk_rows[0])
-        load(gs_sb[0][:, 0, :], gs_rows[0][:, 0, :])
-        load(mk_sb[1][:], mk_rows[1])
-        load(gs_sb[0][:, 1, :], gs_rows[0][:, 1, :])
-        load(gs_sb[1][:, 0, :], gs_rows[1][:, 0, :])
-        load(gs_sb[1][:, 1, :], gs_rows[1][:, 1, :])
+        def prepare_w(h):
+            interleave(nc.scalar.copy, w_bf[h][:], w_raw[h][:])
+            quantize(w_codes[h][:], w_scales[h][:], w_bf[h][:])
 
-        for u in range(2):
-            src = dy_raw[u][:].rearrange("p j n -> p n j")
-            nc.vector.tensor_copy(out=dy_bf[:, :DY_VECTOR_COLS, 2 * u : 2 * u + 2], in_=src[:, :DY_VECTOR_COLS, :])
-            nc.scalar.copy(out=dy_bf[:, DY_VECTOR_COLS:, 2 * u : 2 * u + 2], in_=src[:, DY_VECTOR_COLS:, :])
-        nc.vector.quantize_mx(
-            out=dy_codes[:].bitcast(E5M2X4),
-            scales=dy_scales[:],
-            in_=dy_bf[:].rearrange("p n j -> p (n j)"),
-        )
-
-        w_src = w_raw[:].rearrange("p j (h s) -> p h s j", h=HALVES)
-        for h, cols in enumerate((W0_VECTOR_COLS, W1_VECTOR_COLS)):
-            nc.vector.tensor_copy(out=w_bf[h][:, :cols, :], in_=w_src[:, h, :cols, :])
-            nc.scalar.copy(out=w_bf[h][:, cols:, :], in_=w_src[:, h, cols:, :])
-        for h in range(HALVES):
-            nc.vector.quantize_mx(
-                out=w_codes[h][:].bitcast(E5M2X4),
-                scales=w_scales[h][:],
-                in_=w_bf[h][:].rearrange("p s j -> p (s j)"),
-            )
+        def multiply(h):
             for g in range(G):
                 rows = slice(g * ROWS, (g + 1) * ROWS)
                 nc.tensor.matmul_mx(
@@ -102,6 +87,34 @@ def tile_rows_gback_relu_kernel(tc, dy, w, mk, gs, out):
                     start=True,
                     stop=True,
                 )
+
+        def mask(h, g):
+            nc.vector.tensor_tensor(out=masked[h][:, g, :], in0=z[h][g][:], in1=mk_sb[h][:, g, :], op=MULT)
+
+        def add(h, g, eng, lo=0, hi=N):
+            eng.tensor_tensor(out=res[h][:, g, lo:hi], in0=masked[h][:, g, lo:hi], in1=gs_sb[h][:, g, lo:hi], op=ADD)
+
+        def store(h, g, lo=0, hi=N):
+            nc.sync.dma_start(out=out_rows[h][:, g, lo:hi], in_=res[h][:, g, lo:hi])
+
+        load(w_raw[0][:], w_rows[:, :, :P])
+        for u in range(2):
+            load(dy_raw[u][:], dy_rows[:, :, u * DY_LOAD : (u + 1) * DY_LOAD])
+        load(w_raw[1][:], w_rows[:, :, P:])
+        load(mk_sb[0][:], mk_rows[0])
+        load(gs_sb[0][:, 0, :], gs_rows[0][:, 0, :])
+        load(mk_sb[1][:, 0, :], mk_rows[1][:, 0, :])
+        load(mk_sb[1][:, 1, :], mk_rows[1][:, 1, :])
+        load(gs_sb[0][:, 1, :], gs_rows[0][:, 1, :])
+        load(gs_sb[1][:, 0, :], gs_rows[1][:, 0, :])
+        load(gs_sb[1][:, 1, :], gs_rows[1][:, 1, :])
+
+        prepare_w(0)
+        prepare_dy(0)
+        prepare_dy(1)
+        multiply(0)
+        prepare_w(1)
+        multiply(1)
 
         mask(0, 0)
         add(0, 0, nc.gpsimd)

@@ -109,6 +109,25 @@ def tile_rows_gback_relu_kernel(tc, dy, w, mk, gs, out):
         load(gs_sb[1][:, 0, :], gs_rows[1][:, 0, :])
         load(gs_sb[1][:, 1, :], gs_rows[1][:, 1, :])
 
+        warm_bf = sb.tile([P, N * PACK], BF16, align_bytes=64)
+        warm_codes = sb.tile([P, N], U32, align_bytes=64)
+        warm_scales = sb.tile([P, N], U8, align_bytes=64)
+        warm_out = [psum.tile([P, N], F32, name="warm_out%d" % g) for g in range(G)]
+        nc.vector.memset(warm_bf[:].bitcast(U32), 0)
+        nc.vector.quantize_mx(out=warm_codes[:].bitcast(E5M2X4), scales=warm_scales[:], in_=warm_bf[:])
+        for r in range(8):
+            for g in range(G):
+                rows = slice(g * ROWS, (g + 1) * ROWS)
+                nc.tensor.matmul_mx(
+                    out=warm_out[g][:],
+                    lhsT=warm_codes[rows, :P].bitcast(E5M2X4),
+                    lhsT_scale=warm_scales[rows, :P],
+                    rhs=warm_codes[rows, :].bitcast(E5M2X4),
+                    rhs_scale=warm_scales[rows, :],
+                    start=True,
+                    stop=True,
+                )
+
         prepare_w(0)
         prepare_dy(0)
         prepare_dy(1)

@@ -17,10 +17,11 @@ P = 128
 PACK = 4
 ROWS = D // PACK
 HALVES = M // P
-DY_LOAD = N // 2
 QUANT = 128
-DY_VECTOR_COLS = 168
 RUN = 4
+EARLY = 320
+W_VECTOR_COLS = 168
+EARLY_VECTOR_COLS = 192
 
 
 def tile_rows_gback_relu_kernel(tc, dy, w, mk, gs, out):
@@ -36,60 +37,47 @@ def tile_rows_gback_relu_kernel(tc, dy, w, mk, gs, out):
         psum = ctx.enter_context(tc.psum_pool(name="psum", bufs=1))
         ctx.enter_context(tc.manual_schedule())
 
-        dy_raw = [sb.tile([P, PACK, DY_LOAD], F32, name="dy_raw%d" % u, align_bytes=64) for u in range(2)]
-        w_raw = [sb.tile([P, PACK, P], F32, name="w_raw%d" % h, align_bytes=64) for h in range(HALVES)]
+        dy_early = sb.tile([P, PACK, EARLY], F32, align_bytes=64)
+        dy_late = sb.tile([P, PACK, N - EARLY], F32, align_bytes=64)
+        w_raw = sb.tile([P, PACK, M], F32, align_bytes=64)
         mk_sb = [sb.tile([P, G, N], F32, name="mk%d" % h, align_bytes=64) for h in range(HALVES)]
         gs_sb = [sb.tile([P, G, N], F32, name="gs%d" % h, align_bytes=64) for h in range(HALVES)]
         masked = [sb.tile([P, G, N], F32, name="masked%d" % h, align_bytes=64) for h in range(HALVES)]
         res = [sb.tile([P, G, N], F32, name="res%d" % h, align_bytes=64) for h in range(HALVES)]
-        dy_bf = sb.tile([P, N, PACK], BF16, align_bytes=64)
-        dy_codes = sb.tile([P, N], U32, align_bytes=64)
-        dy_scales = sb.tile([P, N], U8, align_bytes=64)
-        w_bf = [sb.tile([P, P, PACK], BF16, name="w_bf%d" % h, align_bytes=64) for h in range(HALVES)]
-        w_codes = [sb.tile([P, P], U32, name="w_codes%d" % h, align_bytes=64) for h in range(HALVES)]
-        w_scales = [sb.tile([P, P], U8, name="w_scales%d" % h, align_bytes=64) for h in range(HALVES)]
+        values = sb.tile([P, M + N, PACK], BF16, align_bytes=64)
+        codes = sb.tile([P, M + N], U32, align_bytes=64)
+        scales = sb.tile([P, M + N], U8, align_bytes=64)
+        z_early = [psum.tile([P, N], F32, name="z_early%d" % g) for g in range(G)]
         z = [[psum.tile([P, N], F32, name="z%d%d" % (h, g)) for g in range(G)] for h in range(HALVES)]
 
         def load(dst, src):
             nc.sync.dma_start(out=dst, in_=src)
 
-        def interleave(copy, dst, src):
+        def interleave(copy, first, src):
+            dst = values[:, first : first + src.shape[2], :]
             copy(out=dst.rearrange("p (c i) j -> p c j i", i=RUN), in_=src.rearrange("p j (c i) -> p c j i", i=RUN))
 
-        def quantize(codes, scales, values):
-            nc.vector.quantize_mx(out=codes.bitcast(E5M2X4), scales=scales, in_=values.rearrange("p c j -> p (c j)"))
+        def quantize(lo, hi):
+            nc.vector.quantize_mx(
+                out=codes[:, lo:hi].bitcast(E5M2X4),
+                scales=scales[:, lo:hi],
+                in_=values[:, lo:hi, :].rearrange("p c j -> p (c j)"),
+            )
 
-        def prepare_dy(u):
-            base = u * DY_LOAD
-            for copy, lo, hi in (
-                (nc.vector.tensor_copy, 0, QUANT),
-                (nc.vector.tensor_copy, QUANT, DY_VECTOR_COLS),
-                (nc.scalar.copy, DY_VECTOR_COLS, DY_LOAD),
-            ):
-                interleave(copy, dy_bf[:, base + lo : base + hi, :], dy_raw[u][:, :, lo:hi])
-            for lo in range(base, base + DY_LOAD, QUANT):
-                cols = slice(lo, lo + QUANT)
-                quantize(dy_codes[:, cols], dy_scales[:, cols], dy_bf[:, cols, :])
+        def multiply(bank, h, g, first):
+            rows = slice(g * ROWS, (g + 1) * ROWS)
+            nc.tensor.matmul_mx(
+                out=bank[:],
+                lhsT=codes[rows, h * P : (h + 1) * P].bitcast(E5M2X4),
+                lhsT_scale=scales[rows, h * P : (h + 1) * P],
+                rhs=codes[rows, first : first + N].bitcast(E5M2X4),
+                rhs_scale=scales[rows, first : first + N],
+                start=True,
+                stop=True,
+            )
 
-        def prepare_w(h):
-            interleave(nc.scalar.copy, w_bf[h][:], w_raw[h][:])
-            quantize(w_codes[h][:], w_scales[h][:], w_bf[h][:])
-
-        def multiply(h):
-            for g in range(G):
-                rows = slice(g * ROWS, (g + 1) * ROWS)
-                nc.tensor.matmul_mx(
-                    out=z[h][g][:],
-                    lhsT=w_codes[h][rows, :].bitcast(E5M2X4),
-                    lhsT_scale=w_scales[h][rows, :],
-                    rhs=dy_codes[rows, :].bitcast(E5M2X4),
-                    rhs_scale=dy_scales[rows, :],
-                    start=True,
-                    stop=True,
-                )
-
-        def mask(h, g):
-            nc.vector.tensor_tensor(out=masked[h][:, g, :], in0=z[h][g][:], in1=mk_sb[h][:, g, :], op=MULT)
+        def mask(h, g, sums, lo=0, hi=N):
+            nc.vector.tensor_tensor(out=masked[h][:, g, lo:hi], in0=sums, in1=mk_sb[h][:, g, lo:hi], op=MULT)
 
         def add(h, g, eng, lo=0, hi=N):
             eng.tensor_tensor(out=res[h][:, g, lo:hi], in0=masked[h][:, g, lo:hi], in1=gs_sb[h][:, g, lo:hi], op=ADD)
@@ -97,10 +85,9 @@ def tile_rows_gback_relu_kernel(tc, dy, w, mk, gs, out):
         def store(h, g, lo=0, hi=N):
             nc.sync.dma_start(out=out_rows[h][:, g, lo:hi], in_=res[h][:, g, lo:hi])
 
-        load(w_raw[0][:], w_rows[:, :, :P])
-        for u in range(2):
-            load(dy_raw[u][:], dy_rows[:, :, u * DY_LOAD : (u + 1) * DY_LOAD])
-        load(w_raw[1][:], w_rows[:, :, P:])
+        load(w_raw[:], w_rows)
+        load(dy_early[:], dy_rows[:, :, :EARLY])
+        load(dy_late[:], dy_rows[:, :, EARLY:])
         load(mk_sb[0][:], mk_rows[0])
         load(gs_sb[0][:, 0, :], gs_rows[0][:, 0, :])
         load(mk_sb[1][:, 0, :], mk_rows[1][:, 0, :])
@@ -109,38 +96,38 @@ def tile_rows_gback_relu_kernel(tc, dy, w, mk, gs, out):
         load(gs_sb[1][:, 0, :], gs_rows[1][:, 0, :])
         load(gs_sb[1][:, 1, :], gs_rows[1][:, 1, :])
 
-        warm_bf = sb.tile([P, N * PACK], BF16, align_bytes=64)
-        warm_codes = sb.tile([P, N], U32, align_bytes=64)
-        warm_scales = sb.tile([P, N], U8, align_bytes=64)
-        warm_out = [psum.tile([P, N], F32, name="warm_out%d" % g) for g in range(G)]
-        nc.vector.memset(warm_bf[:].bitcast(U32), 0)
-        nc.vector.quantize_mx(out=warm_codes[:].bitcast(E5M2X4), scales=warm_scales[:], in_=warm_bf[:])
-        for r in range(8):
+        interleave(nc.scalar.copy, W_VECTOR_COLS, w_raw[:, :, W_VECTOR_COLS:])
+        interleave(nc.vector.tensor_copy, 0, w_raw[:, :, :W_VECTOR_COLS])
+        quantize(0, M)
+
+        interleave(nc.scalar.copy, M + EARLY_VECTOR_COLS, dy_early[:, :, EARLY_VECTOR_COLS:])
+        interleave(nc.vector.tensor_copy, M, dy_early[:, :, :QUANT])
+        interleave(nc.vector.tensor_copy, M + QUANT, dy_early[:, :, QUANT:EARLY_VECTOR_COLS])
+        quantize(M, M + QUANT)
+        quantize(M + QUANT, M + EARLY - QUANT)
+        quantize(M + EARLY - QUANT, M + EARLY)
+        for g in range(G):
+            multiply(z_early[g], 0, g, M + EARLY - N)
+
+        late = M + EARLY
+        interleave(nc.scalar.copy, late + QUANT, dy_late[:, :, QUANT:])
+        interleave(nc.vector.tensor_copy, late, dy_late[:, :, : QUANT // 2])
+        interleave(nc.vector.tensor_copy, late + QUANT // 2, dy_late[:, :, QUANT // 2 : QUANT])
+        quantize(late, late + QUANT // 2)
+        quantize(late + QUANT // 2, M + N)
+        for h in range(HALVES):
             for g in range(G):
-                rows = slice(g * ROWS, (g + 1) * ROWS)
-                nc.tensor.matmul_mx(
-                    out=warm_out[g][:],
-                    lhsT=warm_codes[rows, :P].bitcast(E5M2X4),
-                    lhsT_scale=warm_scales[rows, :P],
-                    rhs=warm_codes[rows, :].bitcast(E5M2X4),
-                    rhs_scale=warm_scales[rows, :],
-                    start=True,
-                    stop=True,
-                )
+                multiply(z[h][g], h, g, M)
 
-        prepare_w(0)
-        prepare_dy(0)
-        prepare_dy(1)
-        multiply(0)
-        prepare_w(1)
-        multiply(1)
-
-        mask(0, 0)
-        add(0, 0, nc.gpsimd)
+        mask(0, 0, z_early[0][:, N - EARLY :], 0, EARLY)
+        add(0, 0, nc.gpsimd, 0, EARLY)
+        mask(0, 1, z_early[1][:, N - EARLY :], 0, EARLY)
+        mask(0, 0, z[0][0][:, EARLY:], EARLY, N)
+        add(0, 0, nc.gpsimd, EARLY, N)
         store(0, 0)
-        mask(0, 1)
-        mask(1, 0)
-        mask(1, 1)
+        mask(0, 1, z[0][1][:, EARLY:], EARLY, N)
+        mask(1, 0, z[1][0][:])
+        mask(1, 1, z[1][1][:])
         add(0, 1, nc.vector)
         store(0, 1)
         add(1, 0, nc.vector)

@@ -91,9 +91,9 @@ def tile_rows_gback_relu_kernel(tc, dy, w, mk, gs, out):
         load(mk_sb[0][:], mk_rows[0])
         load(gs_sb[0][:, 0, :], gs_rows[0][:, 0, :])
         load(mk_sb[1][:, 0, :], mk_rows[1][:, 0, :])
-        load(mk_sb[1][:, 1, :], mk_rows[1][:, 1, :])
         load(gs_sb[0][:, 1, :], gs_rows[0][:, 1, :])
         load(gs_sb[1][:, 0, :], gs_rows[1][:, 0, :])
+        load(mk_sb[1][:, 1, :], mk_rows[1][:, 1, :])
         load(gs_sb[1][:, 1, :], gs_rows[1][:, 1, :])
 
         interleave(nc.scalar.copy, W_VECTOR_COLS, w_raw[:, :, W_VECTOR_COLS:])
@@ -123,14 +123,16 @@ def tile_rows_gback_relu_kernel(tc, dy, w, mk, gs, out):
         add(0, 0, nc.gpsimd, 0, EARLY)
         mask(0, 1, z_early[1][:, N - EARLY :], 0, EARLY)
         mask(0, 0, z[0][0][:, EARLY:], EARLY, N)
-        add(0, 0, nc.gpsimd, EARLY, N)
-        store(0, 0)
         mask(0, 1, z[0][1][:, EARLY:], EARLY, N)
         mask(1, 0, z[1][0][:])
-        mask(1, 1, z[1][1][:])
+        add(0, 0, nc.vector, EARLY, N)
+        store(0, 0)
         add(0, 1, nc.vector)
         store(0, 1)
         add(1, 0, nc.vector)
         store(1, 0)
-        add(1, 1, nc.vector)
-        store(1, 1)
+        for lo in (0, N // 2):
+            mask(1, 1, z[1][1][:, lo : lo + N // 2], lo, lo + N // 2)
+        for lo in (0, N // 2):
+            add(1, 1, nc.vector, lo, lo + N // 2)
+            store(1, 1, lo, lo + N // 2)

@@ -19,9 +19,10 @@ ROWS = D // PACK
 HALVES = M // P
 QUANT = 128
 RUN = 4
-EARLY = 320
-W_VECTOR_COLS = 168
-EARLY_VECTOR_COLS = 192
+EARLY = N - P
+W_AT = (P, 0)
+W_VECTOR_COLS = 88
+POOL_COLS = 320
 
 
 def tile_rows_gback_relu_kernel(tc, dy, w, mk, gs, out):
@@ -68,8 +69,8 @@ def tile_rows_gback_relu_kernel(tc, dy, w, mk, gs, out):
             rows = slice(g * ROWS, (g + 1) * ROWS)
             nc.tensor.matmul_mx(
                 out=bank[:],
-                lhsT=codes[rows, h * P : (h + 1) * P].bitcast(E5M2X4),
-                lhsT_scale=scales[rows, h * P : (h + 1) * P],
+                lhsT=codes[rows, W_AT[h] : W_AT[h] + P].bitcast(E5M2X4),
+                lhsT_scale=scales[rows, W_AT[h] : W_AT[h] + P],
                 rhs=codes[rows, first : first + N].bitcast(E5M2X4),
                 rhs_scale=scales[rows, first : first + N],
                 start=True,
@@ -85,8 +86,8 @@ def tile_rows_gback_relu_kernel(tc, dy, w, mk, gs, out):
         def store(h, g, lo=0, hi=N):
             nc.sync.dma_start(out=out_rows[h][:, g, lo:hi], in_=res[h][:, g, lo:hi])
 
-        load(w_raw[:], w_rows)
         load(dy_early[:], dy_rows[:, :, :EARLY])
+        load(w_raw[:], w_rows)
         load(dy_late[:], dy_rows[:, :, EARLY:])
         load(mk_sb[0][:], mk_rows[0])
         load(gs_sb[0][:, 0, :], gs_rows[0][:, 0, :])
@@ -96,36 +97,36 @@ def tile_rows_gback_relu_kernel(tc, dy, w, mk, gs, out):
         load(mk_sb[1][:, 1, :], mk_rows[1][:, 1, :])
         load(gs_sb[1][:, 1, :], gs_rows[1][:, 1, :])
 
-        interleave(nc.scalar.copy, W_VECTOR_COLS, w_raw[:, :, W_VECTOR_COLS:])
-        interleave(nc.vector.tensor_copy, 0, w_raw[:, :, :W_VECTOR_COLS])
-        quantize(0, M)
+        interleave(nc.scalar.copy, M + 2 * QUANT, dy_early[:, :, 2 * QUANT :])
+        for lo in (0, QUANT):
+            interleave(nc.vector.tensor_copy, M + lo, dy_early[:, :, lo : lo + QUANT])
+        for lo in range(M, M + EARLY, QUANT):
+            quantize(lo, lo + QUANT)
 
-        interleave(nc.scalar.copy, M + EARLY_VECTOR_COLS, dy_early[:, :, EARLY_VECTOR_COLS:])
-        interleave(nc.vector.tensor_copy, M, dy_early[:, :, :QUANT])
-        interleave(nc.vector.tensor_copy, M + QUANT, dy_early[:, :, QUANT:EARLY_VECTOR_COLS])
-        quantize(M, M + QUANT)
-        quantize(M + QUANT, M + EARLY - QUANT)
-        quantize(M + EARLY - QUANT, M + EARLY)
+        interleave(nc.scalar.copy, W_AT[0] + W_VECTOR_COLS, w_raw[:, :, W_VECTOR_COLS:P])
+        interleave(nc.vector.tensor_copy, W_AT[0], w_raw[:, :, :W_VECTOR_COLS])
+        interleave(nc.scalar.copy, W_AT[1], w_raw[:, :, P:])
+        quantize(W_AT[0], W_AT[0] + P)
         for g in range(G):
-            multiply(z_early[g], 0, g, M + EARLY - N)
+            multiply(z_early[g], 0, g, W_AT[0])
 
         late = M + EARLY
-        interleave(nc.scalar.copy, late + QUANT, dy_late[:, :, QUANT:])
-        interleave(nc.vector.tensor_copy, late, dy_late[:, :, : QUANT // 2])
-        interleave(nc.vector.tensor_copy, late + QUANT // 2, dy_late[:, :, QUANT // 2 : QUANT])
-        quantize(late, late + QUANT // 2)
-        quantize(late + QUANT // 2, M + N)
+        for lo in (0, QUANT // 2):
+            interleave(nc.vector.tensor_copy, late + lo, dy_late[:, :, lo : lo + QUANT // 2])
+        for lo in (0, QUANT // 2):
+            quantize(late + lo, late + lo + QUANT // 2)
+        quantize(W_AT[1], W_AT[1] + P)
         for h in range(HALVES):
             for g in range(G):
                 multiply(z[h][g], h, g, M)
 
         mask(0, 0, z_early[0][:, N - EARLY :], 0, EARLY)
-        add(0, 0, nc.gpsimd, 0, EARLY)
+        add(0, 0, nc.gpsimd, 0, POOL_COLS)
         mask(0, 1, z_early[1][:, N - EARLY :], 0, EARLY)
         mask(0, 0, z[0][0][:, EARLY:], EARLY, N)
         mask(0, 1, z[0][1][:, EARLY:], EARLY, N)
         mask(1, 0, z[1][0][:])
-        add(0, 0, nc.vector, EARLY, N)
+        add(0, 0, nc.vector, POOL_COLS, N)
         store(0, 0)
         add(0, 1, nc.vector)
         store(0, 1)

@@ -21,8 +21,8 @@ QUANT = 128
 RUN = 4
 EARLY = N - P
 W_AT = (P, 0)
-W_VECTOR_COLS = 88
-POOL_COLS = 320
+W_VECTOR_COLS = 80
+POOL_COLS = 384
 
 
 def tile_rows_gback_relu_kernel(tc, dy, w, mk, gs, out):

@@ -86,7 +86,8 @@ def tile_rows_gback_relu_kernel(tc, dy, w, mk, gs, out):
         def store(h, g, lo=0, hi=N):
             nc.sync.dma_start(out=out_rows[h][:, g, lo:hi], in_=res[h][:, g, lo:hi])
 
-        load(dy_early[:], dy_rows[:, :, :EARLY])
+        load(dy_early[:, :1, :], dy_rows[:, :1, :EARLY])
+        load(dy_early[:, 1:, :], dy_rows[:, 1:, :EARLY])
         load(w_raw[:], w_rows)
         load(dy_late[:], dy_rows[:, :, EARLY:])
         load(mk_sb[0][:], mk_rows[0])

@@ -54,8 +54,9 @@ def tile_rows_gback_relu_kernel(tc, dy, w, mk, gs, out):
         def load(dst, src):
             nc.sync.dma_start(out=dst, in_=src)
 
-        def interleave(copy, first, src):
-            dst = values[:, first : first + src.shape[2], :]
+        def interleave(copy, first, src, places=slice(0, PACK)):
+            src = src[:, places, :]
+            dst = values[:, first : first + src.shape[2], places]
             copy(out=dst.rearrange("p (c i) j -> p c j i", i=RUN), in_=src.rearrange("p j (c i) -> p c j i", i=RUN))
 
         def quantize(lo, hi):
@@ -98,9 +99,12 @@ def tile_rows_gback_relu_kernel(tc, dy, w, mk, gs, out):
         load(mk_sb[1][:, 1, :], mk_rows[1][:, 1, :])
         load(gs_sb[1][:, 1, :], gs_rows[1][:, 1, :])
 
-        interleave(nc.scalar.copy, M + 2 * QUANT, dy_early[:, :, 2 * QUANT :])
+        first_row, other_rows = slice(0, 1), slice(1, PACK)
+        interleave(nc.scalar.copy, M + 2 * QUANT, dy_early[:, :, 2 * QUANT :], first_row)
+        interleave(nc.vector.tensor_copy, M, dy_early[:, :, : 2 * QUANT], first_row)
+        interleave(nc.scalar.copy, M + 2 * QUANT, dy_early[:, :, 2 * QUANT :], other_rows)
         for lo in (0, QUANT):
-            interleave(nc.vector.tensor_copy, M + lo, dy_early[:, :, lo : lo + QUANT])
+            interleave(nc.vector.tensor_copy, M + lo, dy_early[:, :, lo : lo + QUANT], other_rows)
         for lo in range(M, M + EARLY, QUANT):
             quantize(lo, lo + QUANT)
 

@@ -21,7 +21,6 @@ QUANT = 128
 RUN = 4
 EARLY = N - P
 W_AT = (P, 0)
-W_VECTOR_COLS = 80
 POOL_COLS = 384
 
 
@@ -108,10 +107,11 @@ def tile_rows_gback_relu_kernel(tc, dy, w, mk, gs, out):
         for lo in range(M, M + EARLY, QUANT):
             quantize(lo, lo + QUANT)
 
-        interleave(nc.scalar.copy, W_AT[0] + W_VECTOR_COLS, w_raw[:, :, W_VECTOR_COLS:P])
-        interleave(nc.vector.tensor_copy, W_AT[0], w_raw[:, :, :W_VECTOR_COLS])
         interleave(nc.scalar.copy, W_AT[1], w_raw[:, :, P:])
-        quantize(W_AT[0], W_AT[0] + P)
+        for lo in (0, QUANT // 2):
+            interleave(nc.vector.tensor_copy, W_AT[0] + lo, w_raw[:, :, lo : lo + QUANT // 2])
+        for lo in (0, QUANT // 2):
+            quantize(W_AT[0] + lo, W_AT[0] + lo + QUANT // 2)
         for g in range(G):
             multiply(z_early[g], 0, g, W_AT[0])
 

@@ -22,6 +22,7 @@ RUN = 4
 EARLY = N - P
 W_AT = (P, 0)
 POOL_COLS = 384
+REUSED = 64
 
 
 def tile_rows_gback_relu_kernel(tc, dy, w, mk, gs, out):
@@ -43,6 +44,8 @@ def tile_rows_gback_relu_kernel(tc, dy, w, mk, gs, out):
         mk_sb = [sb.tile([P, G, N], F32, name="mk%d" % h, align_bytes=64) for h in range(HALVES)]
         gs_sb = [sb.tile([P, G, N], F32, name="gs%d" % h, align_bytes=64) for h in range(HALVES)]
         masked = [sb.tile([P, G, N], F32, name="masked%d" % h, align_bytes=64) for h in range(HALVES)]
+        last = sb.tile([P, N // 2 - REUSED + N], F32, align_bytes=64)
+        mk_last = last[:, N // 2 - REUSED :]
         res = [sb.tile([P, G, N], F32, name="res%d" % h, align_bytes=64) for h in range(HALVES)]
         values = sb.tile([P, M + N, PACK], BF16, align_bytes=64)
         codes = sb.tile([P, M + N], U32, align_bytes=64)
@@ -95,7 +98,7 @@ def tile_rows_gback_relu_kernel(tc, dy, w, mk, gs, out):
         load(mk_sb[1][:, 0, :], mk_rows[1][:, 0, :])
         load(gs_sb[0][:, 1, :], gs_rows[0][:, 1, :])
         load(gs_sb[1][:, 0, :], gs_rows[1][:, 0, :])
-        load(mk_sb[1][:, 1, :], mk_rows[1][:, 1, :])
+        load(mk_last, mk_rows[1][:, 1, :])
         load(gs_sb[1][:, 1, :], gs_rows[1][:, 1, :])
 
         first_row, other_rows = slice(0, 1), slice(1, PACK)
@@ -121,9 +124,8 @@ def tile_rows_gback_relu_kernel(tc, dy, w, mk, gs, out):
         for lo in (0, QUANT // 2):
             quantize(late + lo, late + lo + QUANT // 2)
         quantize(W_AT[1], W_AT[1] + P)
-        for h in range(HALVES):
-            for g in range(G):
-                multiply(z[h][g], h, g, M)
+        for h, g in ((0, 0), (0, 1), (1, 1), (1, 0)):
+            multiply(z[h][g], h, g, M)
 
         mask(0, 0, z_early[0][:, N - EARLY :], 0, EARLY)
         add(0, 0, nc.gpsimd, 0, POOL_COLS)
@@ -137,8 +139,11 @@ def tile_rows_gback_relu_kernel(tc, dy, w, mk, gs, out):
         store(0, 1)
         add(1, 0, nc.vector)
         store(1, 0)
-        for lo in (0, N // 2):
-            mask(1, 1, z[1][1][:, lo : lo + N // 2], lo, lo + N // 2)
-        for lo in (0, N // 2):
-            add(1, 1, nc.vector, lo, lo + N // 2)
-            store(1, 1, lo, lo + N // 2)
+        half = N // 2
+        nc.vector.tensor_tensor(out=masked[1][:, 1, :half], in0=z[1][1][:, :half], in1=mk_last[:, :half], op=MULT)
+        for lo, hi in ((half, N - REUSED), (N - REUSED, N)):
+            nc.vector.tensor_tensor(out=last[:, lo - half : hi - half], in0=z[1][1][:, lo:hi], in1=mk_last[:, lo:hi], op=MULT)
+        add(1, 1, nc.vector, 0, half)
+        store(1, 1, 0, half)
+        nc.vector.tensor_tensor(out=res[1][:, 1, half:], in0=last[:, :half], in1=gs_sb[1][:, 1, half:], op=ADD)
+        store(1, 1, half, N)

@@ -23,6 +23,7 @@ EARLY = N - P
 W_AT = (P, 0)
 POOL_COLS = 384
 REUSED = 64
+POOL_LATE = 128
 
 
 def tile_rows_gback_relu_kernel(tc, dy, w, mk, gs, out):
@@ -46,6 +47,9 @@ def tile_rows_gback_relu_kernel(tc, dy, w, mk, gs, out):
         masked = [sb.tile([P, G, N], F32, name="masked%d" % h, align_bytes=64) for h in range(HALVES)]
         last = sb.tile([P, N // 2 - REUSED + N], F32, align_bytes=64)
         mk_last = last[:, N // 2 - REUSED :]
+        third = sb.tile([P, 2 * N - POOL_LATE], F32, align_bytes=64)
+        res_third = third[:, :N]
+        gs_second = third[:, N - POOL_LATE :]
         res = [sb.tile([P, G, N], F32, name="res%d" % h, align_bytes=64) for h in range(HALVES)]
         values = sb.tile([P, M + N, PACK], BF16, align_bytes=64)
         codes = sb.tile([P, M + N], U32, align_bytes=64)
@@ -96,7 +100,7 @@ def tile_rows_gback_relu_kernel(tc, dy, w, mk, gs, out):
         load(mk_sb[0][:], mk_rows[0])
         load(gs_sb[0][:, 0, :], gs_rows[0][:, 0, :])
         load(mk_sb[1][:, 0, :], mk_rows[1][:, 0, :])
-        load(gs_sb[0][:, 1, :], gs_rows[0][:, 1, :])
+        load(gs_second, gs_rows[0][:, 1, :])
         load(gs_sb[1][:, 0, :], gs_rows[1][:, 0, :])
         load(mk_last, mk_rows[1][:, 1, :])
         load(gs_sb[1][:, 1, :], gs_rows[1][:, 1, :])
@@ -135,10 +139,11 @@ def tile_rows_gback_relu_kernel(tc, dy, w, mk, gs, out):
         mask(1, 0, z[1][0][:])
         add(0, 0, nc.vector, POOL_COLS, N)
         store(0, 0)
-        add(0, 1, nc.vector)
+        nc.vector.tensor_tensor(out=res[0][:, 1, :], in0=masked[0][:, 1, :], in1=gs_second, op=ADD)
         store(0, 1)
-        add(1, 0, nc.vector)
-        store(1, 0)
+        for eng, lo, hi in ((nc.vector, 0, N - POOL_LATE), (nc.gpsimd, N - POOL_LATE, N)):
+            eng.tensor_tensor(out=res_third[:, lo:hi], in0=masked[1][:, 0, lo:hi], in1=gs_sb[1][:, 0, lo:hi], op=ADD)
+        nc.sync.dma_start(out=out_rows[1][:, 0, :], in_=res_third)
         half = N // 2
         nc.vector.tensor_tensor(out=masked[1][:, 1, :half], in0=z[1][1][:, :half], in1=mk_last[:, :half], op=MULT)
         for lo, hi in ((half, N - REUSED), (N - REUSED, N)):

@@ -23,7 +23,7 @@ EARLY = N - P
 W_AT = (P, 0)
 POOL_COLS = 384
 REUSED = 64
-POOL_LATE = 128
+POOL_LATE = 96
 
 
 def tile_rows_gback_relu_kernel(tc, dy, w, mk, gs, out):

@@ -24,6 +24,7 @@ W_AT = (P, 0)
 POOL_COLS = 384
 REUSED = 64
 POOL_LATE = 96
+OVERLAP = 64
 
 
 def tile_rows_gback_relu_kernel(tc, dy, w, mk, gs, out):
@@ -47,9 +48,9 @@ def tile_rows_gback_relu_kernel(tc, dy, w, mk, gs, out):
         masked = [sb.tile([P, G, N], F32, name="masked%d" % h, align_bytes=64) for h in range(HALVES)]
         last = sb.tile([P, N // 2 - REUSED + N], F32, align_bytes=64)
         mk_last = last[:, N // 2 - REUSED :]
-        third = sb.tile([P, 2 * N - POOL_LATE], F32, align_bytes=64)
+        third = sb.tile([P, 2 * N - OVERLAP], F32, align_bytes=64)
         res_third = third[:, :N]
-        gs_second = third[:, N - POOL_LATE :]
+        gs_second = third[:, N - OVERLAP :]
         res = [sb.tile([P, G, N], F32, name="res%d" % h, align_bytes=64) for h in range(HALVES)]
         values = sb.tile([P, M + N, PACK], BF16, align_bytes=64)
         codes = sb.tile([P, M + N], U32, align_bytes=64)

@@ -17,14 +17,15 @@ P = 128
 PACK = 4
 ROWS = D // PACK
 HALVES = M // P
-QUANT = 128
 RUN = 4
-EARLY = N - P
-W_AT = (P, 0)
-POOL_COLS = 384
-REUSED = 64
+EARLY = N // 2
+VEC_EARLY = 192
+VEC_W = 160
+VEC_LATE = 160
 POOL_LATE = 96
+REUSED = 64
 OVERLAP = 64
+ALIGN = 256
 
 
 def tile_rows_gback_relu_kernel(tc, dy, w, mk, gs, out):
@@ -40,29 +41,32 @@ def tile_rows_gback_relu_kernel(tc, dy, w, mk, gs, out):
         psum = ctx.enter_context(tc.psum_pool(name="psum", bufs=1))
         ctx.enter_context(tc.manual_schedule())
 
-        dy_early = sb.tile([P, PACK, EARLY], F32, align_bytes=64)
-        dy_late = sb.tile([P, PACK, N - EARLY], F32, align_bytes=64)
-        w_raw = sb.tile([P, PACK, M], F32, align_bytes=64)
-        mk_sb = [sb.tile([P, G, N], F32, name="mk%d" % h, align_bytes=64) for h in range(HALVES)]
-        gs_sb = [sb.tile([P, G, N], F32, name="gs%d" % h, align_bytes=64) for h in range(HALVES)]
-        masked = [sb.tile([P, G, N], F32, name="masked%d" % h, align_bytes=64) for h in range(HALVES)]
-        last = sb.tile([P, N // 2 - REUSED + N], F32, align_bytes=64)
+        dy_first = sb.tile([P, 1, N], F32, align_bytes=ALIGN)
+        dy_early = sb.tile([P, PACK - 1, EARLY], F32, align_bytes=ALIGN)
+        dy_late = sb.tile([P, PACK - 1, N - EARLY], F32, align_bytes=ALIGN)
+        w_raw = sb.tile([P, PACK, M], F32, align_bytes=ALIGN)
+        mk_first = sb.tile([P, G, N], F32, align_bytes=ALIGN)
+        mk_third = sb.tile([P, N], F32, align_bytes=ALIGN)
+        gs_first = sb.tile([P, N], F32, align_bytes=ALIGN)
+        gs_late = sb.tile([P, G, N], F32, align_bytes=ALIGN)
+        masked = [sb.tile([P, G, N], F32, name="masked%d" % h, align_bytes=ALIGN) for h in range(HALVES)]
+        last = sb.tile([P, N // 2 - REUSED + N], F32, align_bytes=ALIGN)
         mk_last = last[:, N // 2 - REUSED :]
-        third = sb.tile([P, 2 * N - OVERLAP], F32, align_bytes=64)
+        third = sb.tile([P, 2 * N - OVERLAP], F32, align_bytes=ALIGN)
         res_third = third[:, :N]
         gs_second = third[:, N - OVERLAP :]
-        res = [sb.tile([P, G, N], F32, name="res%d" % h, align_bytes=64) for h in range(HALVES)]
-        values = sb.tile([P, M + N, PACK], BF16, align_bytes=64)
-        codes = sb.tile([P, M + N], U32, align_bytes=64)
-        scales = sb.tile([P, M + N], U8, align_bytes=64)
+        res_first = sb.tile([P, G, N], F32, align_bytes=ALIGN)
+        res_last = sb.tile([P, N], F32, align_bytes=ALIGN)
+        values = sb.tile([P, M + N, PACK], BF16, align_bytes=ALIGN)
+        codes = sb.tile([P, M + N], U32, align_bytes=ALIGN)
+        scales = sb.tile([P, M + N], U8, align_bytes=ALIGN)
         z_early = [psum.tile([P, N], F32, name="z_early%d" % g) for g in range(G)]
         z = [[psum.tile([P, N], F32, name="z%d%d" % (h, g)) for g in range(G)] for h in range(HALVES)]
 
         def load(dst, src):
             nc.sync.dma_start(out=dst, in_=src)
 
-        def interleave(copy, first, src, places=slice(0, PACK)):
-            src = src[:, places, :]
+        def interleave(copy, first, src, places):
             dst = values[:, first : first + src.shape[2], places]
             copy(out=dst.rearrange("p (c i) j -> p c j i", i=RUN), in_=src.rearrange("p j (c i) -> p c j i", i=RUN))
 
@@ -77,79 +81,74 @@ def tile_rows_gback_relu_kernel(tc, dy, w, mk, gs, out):
             rows = slice(g * ROWS, (g + 1) * ROWS)
             nc.tensor.matmul_mx(
                 out=bank[:],
-                lhsT=codes[rows, W_AT[h] : W_AT[h] + P].bitcast(E5M2X4),
-                lhsT_scale=scales[rows, W_AT[h] : W_AT[h] + P],
+                lhsT=codes[rows, h * P : (h + 1) * P].bitcast(E5M2X4),
+                lhsT_scale=scales[rows, h * P : (h + 1) * P],
                 rhs=codes[rows, first : first + N].bitcast(E5M2X4),
                 rhs_scale=scales[rows, first : first + N],
                 start=True,
                 stop=True,
             )
 
-        def mask(h, g, sums, lo=0, hi=N):
-            nc.vector.tensor_tensor(out=masked[h][:, g, lo:hi], in0=sums, in1=mk_sb[h][:, g, lo:hi], op=MULT)
+        def combine(eng, op, dst, a, b):
+            eng.tensor_tensor(out=dst, in0=a, in1=b, op=op)
 
-        def add(h, g, eng, lo=0, hi=N):
-            eng.tensor_tensor(out=res[h][:, g, lo:hi], in0=masked[h][:, g, lo:hi], in1=gs_sb[h][:, g, lo:hi], op=ADD)
-
-        def store(h, g, lo=0, hi=N):
-            nc.sync.dma_start(out=out_rows[h][:, g, lo:hi], in_=res[h][:, g, lo:hi])
-
-        load(dy_early[:, :1, :], dy_rows[:, :1, :EARLY])
-        load(dy_early[:, 1:, :], dy_rows[:, 1:, :EARLY])
+        load(dy_first[:], dy_rows[:, :1, :])
+        load(dy_early[:], dy_rows[:, 1:, :EARLY])
         load(w_raw[:], w_rows)
-        load(dy_late[:], dy_rows[:, :, EARLY:])
-        load(mk_sb[0][:], mk_rows[0])
-        load(gs_sb[0][:, 0, :], gs_rows[0][:, 0, :])
-        load(mk_sb[1][:, 0, :], mk_rows[1][:, 0, :])
+        load(dy_late[:], dy_rows[:, 1:, EARLY:])
+        load(mk_first[:], mk_rows[0])
+        load(gs_first[:], gs_rows[0][:, 0, :])
+        load(mk_third[:], mk_rows[1][:, 0, :])
         load(gs_second, gs_rows[0][:, 1, :])
-        load(gs_sb[1][:, 0, :], gs_rows[1][:, 0, :])
+        load(gs_late[:, 0, :], gs_rows[1][:, 0, :])
         load(mk_last, mk_rows[1][:, 1, :])
-        load(gs_sb[1][:, 1, :], gs_rows[1][:, 1, :])
+        load(gs_late[:, 1, :], gs_rows[1][:, 1, :])
 
-        first_row, other_rows = slice(0, 1), slice(1, PACK)
-        interleave(nc.scalar.copy, M + 2 * QUANT, dy_early[:, :, 2 * QUANT :], first_row)
-        interleave(nc.vector.tensor_copy, M, dy_early[:, :, : 2 * QUANT], first_row)
-        interleave(nc.scalar.copy, M + 2 * QUANT, dy_early[:, :, 2 * QUANT :], other_rows)
-        for lo in (0, QUANT):
-            interleave(nc.vector.tensor_copy, M + lo, dy_early[:, :, lo : lo + QUANT], other_rows)
-        for lo in range(M, M + EARLY, QUANT):
-            quantize(lo, lo + QUANT)
+        first_row, other_rows, all_rows = slice(0, 1), slice(1, PACK), slice(0, PACK)
+        vec, act = nc.vector.tensor_copy, nc.scalar.copy
+        late_cut = EARLY + VEC_LATE
+        for copy, lo, hi in ((vec, 0, VEC_EARLY), (act, VEC_EARLY, EARLY), (vec, EARLY, late_cut), (act, late_cut, N)):
+            interleave(copy, M + lo, dy_first[:, :, lo:hi], first_row)
+        interleave(act, M + VEC_EARLY, dy_early[:, :, VEC_EARLY:], other_rows)
+        interleave(vec, M, dy_early[:, :, :P], other_rows)
+        interleave(vec, M + P, dy_early[:, :, P:VEC_EARLY], other_rows)
+        for lo in (0, P):
+            quantize(M + lo, M + lo + P)
 
-        interleave(nc.scalar.copy, W_AT[1], w_raw[:, :, P:])
-        for lo in (0, QUANT // 2):
-            interleave(nc.vector.tensor_copy, W_AT[0] + lo, w_raw[:, :, lo : lo + QUANT // 2])
-        for lo in (0, QUANT // 2):
-            quantize(W_AT[0] + lo, W_AT[0] + lo + QUANT // 2)
+        interleave(act, VEC_W, w_raw[:, :, VEC_W:], all_rows)
+        interleave(vec, 0, w_raw[:, :, :P], all_rows)
+        interleave(vec, P, w_raw[:, :, P:VEC_W], all_rows)
+        for lo in (0, P):
+            quantize(lo, lo + P)
         for g in range(G):
-            multiply(z_early[g], 0, g, W_AT[0])
+            multiply(z_early[g], 0, g, 0)
 
-        late = M + EARLY
-        for lo in (0, QUANT // 2):
-            interleave(nc.vector.tensor_copy, late + lo, dy_late[:, :, lo : lo + QUANT // 2])
-        for lo in (0, QUANT // 2):
-            quantize(late + lo, late + lo + QUANT // 2)
-        quantize(W_AT[1], W_AT[1] + P)
+        interleave(act, M + late_cut, dy_late[:, :, VEC_LATE:], other_rows)
+        interleave(vec, M + EARLY, dy_late[:, :, :P], other_rows)
+        interleave(vec, M + EARLY + P, dy_late[:, :, P:VEC_LATE], other_rows)
+        for lo in (EARLY, EARLY + P):
+            quantize(M + lo, M + lo + P)
         for h, g in ((0, 0), (0, 1), (1, 1), (1, 0)):
             multiply(z[h][g], h, g, M)
 
-        mask(0, 0, z_early[0][:, N - EARLY :], 0, EARLY)
-        add(0, 0, nc.gpsimd, 0, POOL_COLS)
-        mask(0, 1, z_early[1][:, N - EARLY :], 0, EARLY)
-        mask(0, 0, z[0][0][:, EARLY:], EARLY, N)
-        mask(0, 1, z[0][1][:, EARLY:], EARLY, N)
-        mask(1, 0, z[1][0][:])
-        add(0, 0, nc.vector, POOL_COLS, N)
-        store(0, 0)
-        nc.vector.tensor_tensor(out=res[0][:, 1, :], in0=masked[0][:, 1, :], in1=gs_second, op=ADD)
-        store(0, 1)
+        for g in range(G):
+            combine(nc.vector, MULT, masked[0][:, g, :EARLY], z_early[g][:, N - EARLY :], mk_first[:, g, :EARLY])
+        combine(nc.gpsimd, ADD, res_first[:, 0, :EARLY], masked[0][:, 0, :EARLY], gs_first[:, :EARLY])
+        for g in range(G):
+            combine(nc.vector, MULT, masked[0][:, g, EARLY:], z[0][g][:, EARLY:], mk_first[:, g, EARLY:])
+        combine(nc.vector, MULT, masked[1][:, 0, :], z[1][0][:], mk_third[:])
+        combine(nc.vector, ADD, res_first[:, 0, EARLY:], masked[0][:, 0, EARLY:], gs_first[:, EARLY:])
+        nc.sync.dma_start(out=out_rows[0][:, 0, :], in_=res_first[:, 0, :])
+        combine(nc.vector, ADD, res_first[:, 1, :], masked[0][:, 1, :], gs_second)
+        nc.sync.dma_start(out=out_rows[0][:, 1, :], in_=res_first[:, 1, :])
         for eng, lo, hi in ((nc.vector, 0, N - POOL_LATE), (nc.gpsimd, N - POOL_LATE, N)):
-            eng.tensor_tensor(out=res_third[:, lo:hi], in0=masked[1][:, 0, lo:hi], in1=gs_sb[1][:, 0, lo:hi], op=ADD)
+            combine(eng, ADD, res_third[:, lo:hi], masked[1][:, 0, lo:hi], gs_late[:, 0, lo:hi])
         nc.sync.dma_start(out=out_rows[1][:, 0, :], in_=res_third)
         half = N // 2
-        nc.vector.tensor_tensor(out=masked[1][:, 1, :half], in0=z[1][1][:, :half], in1=mk_last[:, :half], op=MULT)
+        combine(nc.vector, MULT, masked[1][:, 1, :half], z[1][1][:, :half], mk_last[:, :half])
         for lo, hi in ((half, N - REUSED), (N - REUSED, N)):
-            nc.vector.tensor_tensor(out=last[:, lo - half : hi - half], in0=z[1][1][:, lo:hi], in1=mk_last[:, lo:hi], op=MULT)
-        add(1, 1, nc.vector, 0, half)
-        store(1, 1, 0, half)
-        nc.vector.tensor_tensor(out=res[1][:, 1, half:], in0=last[:, :half], in1=gs_sb[1][:, 1, half:], op=ADD)
-        store(1, 1, half, N)
+            combine(nc.vector, MULT, last[:, lo - half : hi - half], z[1][1][:, lo:hi], mk_last[:, lo:hi])
+        combine(nc.vector, ADD, res_last[:, :half], masked[1][:, 1, :half], gs_late[:, 1, :half])
+        nc.sync.dma_start(out=out_rows[1][:, 1, :half], in_=res_last[:, :half])
+        combine(nc.vector, ADD, res_last[:, half:], last[:, :half], gs_late[:, 1, half:])
+        nc.sync.dma_start(out=out_rows[1][:, 1, half:], in_=res_last[:, half:])

@@ -18,10 +18,11 @@ PACK = 4
 ROWS = D // PACK
 HALVES = M // P
 RUN = 4
-EARLY = N // 2
-VEC_EARLY = 192
-VEC_W = 160
-VEC_LATE = 160
+EARLY = N - P
+W_AT = (P, 0)
+VEC_EARLY = 256
+VEC_W = 96
+POOL_COLS = 384
 POOL_LATE = 96
 REUSED = 64
 OVERLAP = 64
@@ -41,9 +42,9 @@ def tile_rows_gback_relu_kernel(tc, dy, w, mk, gs, out):
         psum = ctx.enter_context(tc.psum_pool(name="psum", bufs=1))
         ctx.enter_context(tc.manual_schedule())
 
-        dy_first = sb.tile([P, 1, N], F32, align_bytes=ALIGN)
-        dy_early = sb.tile([P, PACK - 1, EARLY], F32, align_bytes=ALIGN)
-        dy_late = sb.tile([P, PACK - 1, N - EARLY], F32, align_bytes=ALIGN)
+        dy_first = sb.tile([P, PACK - 1, N], F32, align_bytes=ALIGN)
+        dy_early = sb.tile([P, 1, EARLY], F32, align_bytes=ALIGN)
+        dy_late = sb.tile([P, 1, N - EARLY], F32, align_bytes=ALIGN)
         w_raw = sb.tile([P, PACK, M], F32, align_bytes=ALIGN)
         mk_first = sb.tile([P, G, N], F32, align_bytes=ALIGN)
         mk_third = sb.tile([P, N], F32, align_bytes=ALIGN)
@@ -81,8 +82,8 @@ def tile_rows_gback_relu_kernel(tc, dy, w, mk, gs, out):
             rows = slice(g * ROWS, (g + 1) * ROWS)
             nc.tensor.matmul_mx(
                 out=bank[:],
-                lhsT=codes[rows, h * P : (h + 1) * P].bitcast(E5M2X4),
-                lhsT_scale=scales[rows, h * P : (h + 1) * P],
+                lhsT=codes[rows, W_AT[h] : W_AT[h] + P].bitcast(E5M2X4),
+                lhsT_scale=scales[rows, W_AT[h] : W_AT[h] + P],
                 rhs=codes[rows, first : first + N].bitcast(E5M2X4),
                 rhs_scale=scales[rows, first : first + N],
                 start=True,
@@ -92,10 +93,11 @@ def tile_rows_gback_relu_kernel(tc, dy, w, mk, gs, out):
         def combine(eng, op, dst, a, b):
             eng.tensor_tensor(out=dst, in0=a, in1=b, op=op)
 
-        load(dy_first[:], dy_rows[:, :1, :])
-        load(dy_early[:], dy_rows[:, 1:, :EARLY])
+        last_row = PACK - 1
+        load(dy_first[:], dy_rows[:, :last_row, :])
+        load(dy_early[:], dy_rows[:, last_row:, :EARLY])
         load(w_raw[:], w_rows)
-        load(dy_late[:], dy_rows[:, 1:, EARLY:])
+        load(dy_late[:], dy_rows[:, last_row:, EARLY:])
         load(mk_first[:], mk_rows[0])
         load(gs_first[:], gs_rows[0][:, 0, :])
         load(mk_third[:], mk_rows[1][:, 0, :])
@@ -104,40 +106,40 @@ def tile_rows_gback_relu_kernel(tc, dy, w, mk, gs, out):
         load(mk_last, mk_rows[1][:, 1, :])
         load(gs_late[:, 1, :], gs_rows[1][:, 1, :])
 
-        first_row, other_rows, all_rows = slice(0, 1), slice(1, PACK), slice(0, PACK)
+        first_rows, final_row, all_rows = slice(0, last_row), slice(last_row, PACK), slice(0, PACK)
         vec, act = nc.vector.tensor_copy, nc.scalar.copy
-        late_cut = EARLY + VEC_LATE
-        for copy, lo, hi in ((vec, 0, VEC_EARLY), (act, VEC_EARLY, EARLY), (vec, EARLY, late_cut), (act, late_cut, N)):
-            interleave(copy, M + lo, dy_first[:, :, lo:hi], first_row)
-        interleave(act, M + VEC_EARLY, dy_early[:, :, VEC_EARLY:], other_rows)
-        interleave(vec, M, dy_early[:, :, :P], other_rows)
-        interleave(vec, M + P, dy_early[:, :, P:VEC_EARLY], other_rows)
-        for lo in (0, P):
-            quantize(M + lo, M + lo + P)
-
-        interleave(act, VEC_W, w_raw[:, :, VEC_W:], all_rows)
-        interleave(vec, 0, w_raw[:, :, :P], all_rows)
-        interleave(vec, P, w_raw[:, :, P:VEC_W], all_rows)
-        for lo in (0, P):
+        interleave(act, M + VEC_EARLY, dy_first[:, :, VEC_EARLY:EARLY], first_rows)
+        interleave(vec, M, dy_first[:, :, :VEC_EARLY], first_rows)
+        interleave(act, M + VEC_EARLY, dy_early[:, :, VEC_EARLY:], final_row)
+        interleave(act, M + EARLY, dy_first[:, :, EARLY:], first_rows)
+        for lo in range(0, VEC_EARLY, P):
+            interleave(vec, M + lo, dy_early[:, :, lo : lo + P], final_row)
+        for lo in range(M, M + EARLY, P):
             quantize(lo, lo + P)
-        for g in range(G):
-            multiply(z_early[g], 0, g, 0)
 
-        interleave(act, M + late_cut, dy_late[:, :, VEC_LATE:], other_rows)
-        interleave(vec, M + EARLY, dy_late[:, :, :P], other_rows)
-        interleave(vec, M + EARLY + P, dy_late[:, :, P:VEC_LATE], other_rows)
-        for lo in (EARLY, EARLY + P):
-            quantize(M + lo, M + lo + P)
+        quarter = P // 2
+        interleave(act, W_AT[0] + VEC_W, w_raw[:, :, VEC_W:P], all_rows)
+        interleave(act, M + EARLY, dy_late[:], final_row)
+        interleave(act, W_AT[1] + quarter, w_raw[:, :, P + quarter :], all_rows)
+        interleave(vec, W_AT[0], w_raw[:, :, :quarter], all_rows)
+        interleave(vec, W_AT[0] + quarter, w_raw[:, :, quarter:VEC_W], all_rows)
+        interleave(vec, W_AT[1], w_raw[:, :, P : P + quarter], all_rows)
+        for lo in (0, quarter):
+            quantize(W_AT[0] + lo, W_AT[0] + lo + quarter)
+        for g in range(G):
+            multiply(z_early[g], 0, g, W_AT[0])
+        quantize(M + EARLY, M + N)
+        quantize(W_AT[1], W_AT[1] + P)
         for h, g in ((0, 0), (0, 1), (1, 1), (1, 0)):
             multiply(z[h][g], h, g, M)
 
-        for g in range(G):
-            combine(nc.vector, MULT, masked[0][:, g, :EARLY], z_early[g][:, N - EARLY :], mk_first[:, g, :EARLY])
-        combine(nc.gpsimd, ADD, res_first[:, 0, :EARLY], masked[0][:, 0, :EARLY], gs_first[:, :EARLY])
+        combine(nc.vector, MULT, masked[0][:, 0, :EARLY], z_early[0][:, N - EARLY :], mk_first[:, 0, :EARLY])
+        combine(nc.gpsimd, ADD, res_first[:, 0, :POOL_COLS], masked[0][:, 0, :POOL_COLS], gs_first[:, :POOL_COLS])
+        combine(nc.vector, MULT, masked[0][:, 1, :EARLY], z_early[1][:, N - EARLY :], mk_first[:, 1, :EARLY])
         for g in range(G):
             combine(nc.vector, MULT, masked[0][:, g, EARLY:], z[0][g][:, EARLY:], mk_first[:, g, EARLY:])
         combine(nc.vector, MULT, masked[1][:, 0, :], z[1][0][:], mk_third[:])
-        combine(nc.vector, ADD, res_first[:, 0, EARLY:], masked[0][:, 0, EARLY:], gs_first[:, EARLY:])
+        combine(nc.vector, ADD, res_first[:, 0, POOL_COLS:], masked[0][:, 0, POOL_COLS:], gs_first[:, POOL_COLS:])
         nc.sync.dma_start(out=out_rows[0][:, 0, :], in_=res_first[:, 0, :])
         combine(nc.vector, ADD, res_first[:, 1, :], masked[0][:, 1, :], gs_second)
         nc.sync.dma_start(out=out_rows[0][:, 1, :], in_=res_first[:, 1, :])

@@ -20,8 +20,10 @@ HALVES = M // P
 RUN = 4
 EARLY = N - P
 W_AT = (P, 0)
+FIRST_ROWS = 2
 VEC_EARLY = 256
-VEC_W = 96
+VEC_W = 80
+VEC_W_SECOND = 32
 POOL_COLS = 384
 POOL_LATE = 96
 REUSED = 64
@@ -42,9 +44,9 @@ def tile_rows_gback_relu_kernel(tc, dy, w, mk, gs, out):
         psum = ctx.enter_context(tc.psum_pool(name="psum", bufs=1))
         ctx.enter_context(tc.manual_schedule())
 
-        dy_first = sb.tile([P, PACK - 1, N], F32, align_bytes=ALIGN)
-        dy_early = sb.tile([P, 1, EARLY], F32, align_bytes=ALIGN)
-        dy_late = sb.tile([P, 1, N - EARLY], F32, align_bytes=ALIGN)
+        dy_first = sb.tile([P, FIRST_ROWS, N], F32, align_bytes=ALIGN)
+        dy_early = sb.tile([P, PACK - FIRST_ROWS, EARLY], F32, align_bytes=ALIGN)
+        dy_late = sb.tile([P, PACK - FIRST_ROWS, N - EARLY], F32, align_bytes=ALIGN)
         w_raw = sb.tile([P, PACK, M], F32, align_bytes=ALIGN)
         mk_first = sb.tile([P, G, N], F32, align_bytes=ALIGN)
         mk_third = sb.tile([P, N], F32, align_bytes=ALIGN)
@@ -93,11 +95,10 @@ def tile_rows_gback_relu_kernel(tc, dy, w, mk, gs, out):
         def combine(eng, op, dst, a, b):
             eng.tensor_tensor(out=dst, in0=a, in1=b, op=op)
 
-        last_row = PACK - 1
-        load(dy_first[:], dy_rows[:, :last_row, :])
-        load(dy_early[:], dy_rows[:, last_row:, :EARLY])
+        load(dy_first[:], dy_rows[:, :FIRST_ROWS, :])
+        load(dy_early[:], dy_rows[:, FIRST_ROWS:, :EARLY])
         load(w_raw[:], w_rows)
-        load(dy_late[:], dy_rows[:, last_row:, EARLY:])
+        load(dy_late[:], dy_rows[:, FIRST_ROWS:, EARLY:])
         load(mk_first[:], mk_rows[0])
         load(gs_first[:], gs_rows[0][:, 0, :])
         load(mk_third[:], mk_rows[1][:, 0, :])
@@ -106,28 +107,27 @@ def tile_rows_gback_relu_kernel(tc, dy, w, mk, gs, out):
         load(mk_last, mk_rows[1][:, 1, :])
         load(gs_late[:, 1, :], gs_rows[1][:, 1, :])
 
-        first_rows, final_row, all_rows = slice(0, last_row), slice(last_row, PACK), slice(0, PACK)
+        first_rows, other_rows, all_rows = slice(0, FIRST_ROWS), slice(FIRST_ROWS, PACK), slice(0, PACK)
         vec, act = nc.vector.tensor_copy, nc.scalar.copy
-        interleave(act, M + VEC_EARLY, dy_first[:, :, VEC_EARLY:EARLY], first_rows)
+        quarter = P // 2
         interleave(vec, M, dy_first[:, :, :VEC_EARLY], first_rows)
-        interleave(act, M + VEC_EARLY, dy_early[:, :, VEC_EARLY:], final_row)
-        interleave(act, M + EARLY, dy_first[:, :, EARLY:], first_rows)
-        for lo in range(0, VEC_EARLY, P):
-            interleave(vec, M + lo, dy_early[:, :, lo : lo + P], final_row)
+        interleave(act, M + VEC_EARLY, dy_first[:, :, VEC_EARLY:], first_rows)
+        for lo, hi in ((0, P), (P, VEC_EARLY)):
+            interleave(vec, M + lo, dy_early[:, :, lo:hi], other_rows)
+        interleave(act, M + VEC_EARLY, dy_early[:, :, VEC_EARLY:], other_rows)
         for lo in range(M, M + EARLY, P):
             quantize(lo, lo + P)
 
-        quarter = P // 2
         interleave(act, W_AT[0] + VEC_W, w_raw[:, :, VEC_W:P], all_rows)
-        interleave(act, M + EARLY, dy_late[:], final_row)
-        interleave(act, W_AT[1] + quarter, w_raw[:, :, P + quarter :], all_rows)
+        interleave(act, W_AT[1] + VEC_W_SECOND, w_raw[:, :, P + VEC_W_SECOND :], all_rows)
         interleave(vec, W_AT[0], w_raw[:, :, :quarter], all_rows)
         interleave(vec, W_AT[0] + quarter, w_raw[:, :, quarter:VEC_W], all_rows)
-        interleave(vec, W_AT[1], w_raw[:, :, P : P + quarter], all_rows)
         for lo in (0, quarter):
             quantize(W_AT[0] + lo, W_AT[0] + lo + quarter)
         for g in range(G):
             multiply(z_early[g], 0, g, W_AT[0])
+        interleave(vec, M + EARLY, dy_late[:], other_rows)
+        interleave(vec, W_AT[1], w_raw[:, :, P : P + VEC_W_SECOND], all_rows)
         quantize(M + EARLY, M + N)
         quantize(W_AT[1], W_AT[1] + P)
         for h, g in ((0, 0), (0, 1), (1, 1), (1, 0)):

@@ -23,7 +23,7 @@ W_AT = (P, 0)
 FIRST_ROWS = 2
 VEC_EARLY = 256
 VEC_W = 80
-VEC_W_SECOND = 32
+VEC_W_SECOND = 96
 POOL_COLS = 384
 POOL_LATE = 96
 REUSED = 64
@@ -120,13 +120,13 @@ def tile_rows_gback_relu_kernel(tc, dy, w, mk, gs, out):
 
         interleave(act, W_AT[0] + VEC_W, w_raw[:, :, VEC_W:P], all_rows)
         interleave(act, W_AT[1] + VEC_W_SECOND, w_raw[:, :, P + VEC_W_SECOND :], all_rows)
+        interleave(act, M + EARLY, dy_late[:], other_rows)
         interleave(vec, W_AT[0], w_raw[:, :, :quarter], all_rows)
         interleave(vec, W_AT[0] + quarter, w_raw[:, :, quarter:VEC_W], all_rows)
         for lo in (0, quarter):
             quantize(W_AT[0] + lo, W_AT[0] + lo + quarter)
         for g in range(G):
             multiply(z_early[g], 0, g, W_AT[0])
-        interleave(vec, M + EARLY, dy_late[:], other_rows)
         interleave(vec, W_AT[1], w_raw[:, :, P : P + VEC_W_SECOND], all_rows)
         quantize(M + EARLY, M + N)
         quantize(W_AT[1], W_AT[1] + P)

@@ -19,14 +19,14 @@ ROWS = D // PACK
 HALVES = M // P
 RUN = 4
 EARLY = N - P
-W_AT = (P, 0)
-FIRST_ROWS = 2
+W_AT = (0, P + N)
+DY_AT = P
+PAIR = 2
 VEC_EARLY = 256
 VEC_W = 80
-VEC_W_SECOND = 96
+VEC_W_SECOND = 112
 POOL_COLS = 384
-POOL_LATE = 96
-REUSED = 64
+POOL_LATE = 128
 OVERLAP = 64
 ALIGN = 256
 
@@ -44,17 +44,15 @@ def tile_rows_gback_relu_kernel(tc, dy, w, mk, gs, out):
         psum = ctx.enter_context(tc.psum_pool(name="psum", bufs=1))
         ctx.enter_context(tc.manual_schedule())
 
-        dy_first = sb.tile([P, FIRST_ROWS, N], F32, align_bytes=ALIGN)
-        dy_early = sb.tile([P, PACK - FIRST_ROWS, EARLY], F32, align_bytes=ALIGN)
-        dy_late = sb.tile([P, PACK - FIRST_ROWS, N - EARLY], F32, align_bytes=ALIGN)
+        dy_pair = [sb.tile([P, PAIR, N], F32, name="dy%d" % i, align_bytes=ALIGN) for i in range(PACK // PAIR)]
+        dy_late = sb.tile([P, PACK // PAIR, N - EARLY], F32, align_bytes=ALIGN)
         w_raw = sb.tile([P, PACK, M], F32, align_bytes=ALIGN)
         mk_first = sb.tile([P, G, N], F32, align_bytes=ALIGN)
         mk_third = sb.tile([P, N], F32, align_bytes=ALIGN)
         gs_first = sb.tile([P, N], F32, align_bytes=ALIGN)
         gs_late = sb.tile([P, G, N], F32, align_bytes=ALIGN)
         masked = [sb.tile([P, G, N], F32, name="masked%d" % h, align_bytes=ALIGN) for h in range(HALVES)]
-        last = sb.tile([P, N // 2 - REUSED + N], F32, align_bytes=ALIGN)
-        mk_last = last[:, N // 2 - REUSED :]
+        mk_last = sb.tile([P, N], F32, align_bytes=ALIGN)
         third = sb.tile([P, 2 * N - OVERLAP], F32, align_bytes=ALIGN)
         res_third = third[:, :N]
         gs_second = third[:, N - OVERLAP :]
@@ -95,32 +93,35 @@ def tile_rows_gback_relu_kernel(tc, dy, w, mk, gs, out):
         def combine(eng, op, dst, a, b):
             eng.tensor_tensor(out=dst, in0=a, in1=b, op=op)
 
-        load(dy_first[:], dy_rows[:, :FIRST_ROWS, :])
-        load(dy_early[:], dy_rows[:, FIRST_ROWS:, :EARLY])
+        dy_runs = dy_rows.rearrange("p (i j) n -> p i (j n)", j=PAIR)
+        for i in range(PACK // PAIR):
+            load(dy_pair[i][:].rearrange("p j n -> p (j n)")[:, : N + EARLY], dy_runs[:, i, : N + EARLY])
         load(w_raw[:], w_rows)
-        load(dy_late[:], dy_rows[:, FIRST_ROWS:, EARLY:])
+        load(dy_late[:], dy_runs[:, :, N + EARLY :])
         load(mk_first[:], mk_rows[0])
         load(gs_first[:], gs_rows[0][:, 0, :])
         load(mk_third[:], mk_rows[1][:, 0, :])
         load(gs_second, gs_rows[0][:, 1, :])
         load(gs_late[:, 0, :], gs_rows[1][:, 0, :])
-        load(mk_last, mk_rows[1][:, 1, :])
+        load(mk_last[:], mk_rows[1][:, 1, :])
         load(gs_late[:, 1, :], gs_rows[1][:, 1, :])
 
-        first_rows, other_rows, all_rows = slice(0, FIRST_ROWS), slice(FIRST_ROWS, PACK), slice(0, PACK)
+        first_rows, other_rows, all_rows = slice(0, PAIR), slice(PAIR, PACK), slice(0, PACK)
         vec, act = nc.vector.tensor_copy, nc.scalar.copy
         quarter = P // 2
-        interleave(vec, M, dy_first[:, :, :VEC_EARLY], first_rows)
-        interleave(act, M + VEC_EARLY, dy_first[:, :, VEC_EARLY:], first_rows)
+        interleave(vec, DY_AT, dy_pair[0][:, :, :VEC_EARLY], first_rows)
+        interleave(act, DY_AT + VEC_EARLY, dy_pair[0][:, :, VEC_EARLY:EARLY], first_rows)
+        interleave(act, DY_AT + EARLY, dy_pair[0][:, :1, EARLY:], slice(0, 1))
         for lo, hi in ((0, P), (P, VEC_EARLY)):
-            interleave(vec, M + lo, dy_early[:, :, lo:hi], other_rows)
-        interleave(act, M + VEC_EARLY, dy_early[:, :, VEC_EARLY:], other_rows)
-        for lo in range(M, M + EARLY, P):
+            interleave(vec, DY_AT + lo, dy_pair[1][:, :, lo:hi], other_rows)
+        interleave(act, DY_AT + VEC_EARLY, dy_pair[1][:, :, VEC_EARLY:EARLY], other_rows)
+        interleave(act, DY_AT + EARLY, dy_pair[1][:, :1, EARLY:], slice(PAIR, PAIR + 1))
+        for lo in range(DY_AT, DY_AT + EARLY, P):
             quantize(lo, lo + P)
 
         interleave(act, W_AT[0] + VEC_W, w_raw[:, :, VEC_W:P], all_rows)
         interleave(act, W_AT[1] + VEC_W_SECOND, w_raw[:, :, P + VEC_W_SECOND :], all_rows)
-        interleave(act, M + EARLY, dy_late[:], other_rows)
+        interleave(act, DY_AT + EARLY, dy_late[:], slice(1, PACK, PAIR))
         interleave(vec, W_AT[0], w_raw[:, :, :quarter], all_rows)
         interleave(vec, W_AT[0] + quarter, w_raw[:, :, quarter:VEC_W], all_rows)
         for lo in (0, quarter):
@@ -128,10 +129,10 @@ def tile_rows_gback_relu_kernel(tc, dy, w, mk, gs, out):
         for g in range(G):
             multiply(z_early[g], 0, g, W_AT[0])
         interleave(vec, W_AT[1], w_raw[:, :, P : P + VEC_W_SECOND], all_rows)
-        quantize(M + EARLY, M + N)
+        quantize(DY_AT + EARLY, DY_AT + N)
         quantize(W_AT[1], W_AT[1] + P)
         for h, g in ((0, 0), (0, 1), (1, 1), (1, 0)):
-            multiply(z[h][g], h, g, M)
+            multiply(z[h][g], h, g, DY_AT)
 
         combine(nc.vector, MULT, masked[0][:, 0, :EARLY], z_early[0][:, N - EARLY :], mk_first[:, 0, :EARLY])
         combine(nc.gpsimd, ADD, res_first[:, 0, :POOL_COLS], masked[0][:, 0, :POOL_COLS], gs_first[:, :POOL_COLS])
@@ -147,10 +148,9 @@ def tile_rows_gback_relu_kernel(tc, dy, w, mk, gs, out):
             combine(eng, ADD, res_third[:, lo:hi], masked[1][:, 0, lo:hi], gs_late[:, 0, lo:hi])
         nc.sync.dma_start(out=out_rows[1][:, 0, :], in_=res_third)
         half = N // 2
-        combine(nc.vector, MULT, masked[1][:, 1, :half], z[1][1][:, :half], mk_last[:, :half])
-        for lo, hi in ((half, N - REUSED), (N - REUSED, N)):
-            combine(nc.vector, MULT, last[:, lo - half : hi - half], z[1][1][:, lo:hi], mk_last[:, lo:hi])
+        for lo in (0, half):
+            combine(nc.vector, MULT, masked[1][:, 1, lo : lo + half], z[1][1][:, lo : lo + half], mk_last[:, lo : lo + half])
         combine(nc.vector, ADD, res_last[:, :half], masked[1][:, 1, :half], gs_late[:, 1, :half])
         nc.sync.dma_start(out=out_rows[1][:, 1, :half], in_=res_last[:, :half])
-        combine(nc.vector, ADD, res_last[:, half:], last[:, :half], gs_late[:, 1, half:])
+        combine(nc.vector, ADD, res_last[:, half:], masked[1][:, 1, half:], gs_late[:, 1, half:])
         nc.sync.dma_start(out=out_rows[1][:, 1, half:], in_=res_last[:, half:])

@@ -131,8 +131,9 @@ def tile_rows_gback_relu_kernel(tc, dy, w, mk, gs, out):
         interleave(vec, W_AT[1], w_raw[:, :, P : P + VEC_W_SECOND], all_rows)
         quantize(DY_AT + EARLY, DY_AT + N)
         quantize(W_AT[1], W_AT[1] + P)
-        for h, g in ((0, 0), (0, 1), (1, 1), (1, 0)):
-            multiply(z[h][g], h, g, DY_AT)
+        for h in range(HALVES):
+            for g in range(G):
+                multiply(z[h][g], h, g, DY_AT)
 
         combine(nc.vector, MULT, masked[0][:, 0, :EARLY], z_early[0][:, N - EARLY :], mk_first[:, 0, :EARLY])
         combine(nc.gpsimd, ADD, res_first[:, 0, :POOL_COLS], masked[0][:, 0, :POOL_COLS], gs_first[:, :POOL_COLS])

from contextlib import ExitStack

import concourse.mybir as mybir

G, D, M, N = 2, 256, 256, 512
FLOPS = 2 * G * D * M * N

F32 = mybir.dt.float32
BF16 = mybir.dt.bfloat16
U32 = mybir.dt.uint32
U8 = mybir.dt.uint8
E5M2X4 = mybir.dt.float8_e5m2_x4
MULT = mybir.AluOpType.mult
ADD = mybir.AluOpType.add

P = 128
PACK = 4
ROWS = D // PACK
HALVES = M // P
RUN = 4
EARLY = N - P
W_AT = (0, P + N)
DY_AT = P
PAIR = 2
VEC_EARLY = 256
VEC_W = 80
VEC_W_SECOND = 112
POOL_COLS = 384
POOL_LATE = 128
OVERLAP = 64
ALIGN = 256


def tile_rows_gback_relu_kernel(tc, dy, w, mk, gs, out):
    nc = tc.nc
    dy_rows = dy.rearrange("g (p j) n -> (g p) j n", j=PACK)
    w_rows = w.rearrange("g (p j) m -> (g p) j m", j=PACK)
    mk_rows = mk.rearrange("g (h p) n -> h p g n", h=HALVES)
    gs_rows = gs.rearrange("g (h p) n -> h p g n", h=HALVES)
    out_rows = out.rearrange("g (h p) n -> h p g n", h=HALVES)

    with ExitStack() as ctx:
        sb = ctx.enter_context(tc.tile_pool(name="sb", bufs=1))
        psum = ctx.enter_context(tc.psum_pool(name="psum", bufs=1))
        ctx.enter_context(tc.manual_schedule())

        dy_pair = [sb.tile([P, PAIR, N], F32, name="dy%d" % i, align_bytes=ALIGN) for i in range(PACK // PAIR)]
        dy_late = sb.tile([P, PACK // PAIR, N - EARLY], F32, align_bytes=ALIGN)
        w_raw = sb.tile([P, PACK, M], F32, align_bytes=ALIGN)
        mk_first = sb.tile([P, G, N], F32, align_bytes=ALIGN)
        mk_third = sb.tile([P, N], F32, align_bytes=ALIGN)
        gs_first = sb.tile([P, N], F32, align_bytes=ALIGN)
        gs_late = sb.tile([P, G, N], F32, align_bytes=ALIGN)
        masked = [sb.tile([P, G, N], F32, name="masked%d" % h, align_bytes=ALIGN) for h in range(HALVES)]
        mk_last = sb.tile([P, N], F32, align_bytes=ALIGN)
        third = sb.tile([P, 2 * N - OVERLAP], F32, align_bytes=ALIGN)
        res_third = third[:, :N]
        gs_second = third[:, N - OVERLAP :]
        res_first = sb.tile([P, G, N], F32, align_bytes=ALIGN)
        res_last = sb.tile([P, N], F32, align_bytes=ALIGN)
        values = sb.tile([P, M + N, PACK], BF16, align_bytes=ALIGN)
        codes = sb.tile([P, M + N], U32, align_bytes=ALIGN)
        scales = sb.tile([P, M + N], U8, align_bytes=ALIGN)
        z_early = [psum.tile([P, N], F32, name="z_early%d" % g) for g in range(G)]
        z = [[psum.tile([P, N], F32, name="z%d%d" % (h, g)) for g in range(G)] for h in range(HALVES)]

        def load(dst, src):
            nc.sync.dma_start(out=dst, in_=src)

        def interleave(copy, first, src, places):
            dst = values[:, first : first + src.shape[2], places]
            copy(out=dst.rearrange("p (c i) j -> p c j i", i=RUN), in_=src.rearrange("p j (c i) -> p c j i", i=RUN))

        def quantize(lo, hi):
            nc.vector.quantize_mx(
                out=codes[:, lo:hi].bitcast(E5M2X4),
                scales=scales[:, lo:hi],
                in_=values[:, lo:hi, :].rearrange("p c j -> p (c j)"),
            )

        def multiply(bank, h, g, first):
            rows = slice(g * ROWS, (g + 1) * ROWS)
            nc.tensor.matmul_mx(
                out=bank[:],
                lhsT=codes[rows, W_AT[h] : W_AT[h] + P].bitcast(E5M2X4),
                lhsT_scale=scales[rows, W_AT[h] : W_AT[h] + P],
                rhs=codes[rows, first : first + N].bitcast(E5M2X4),
                rhs_scale=scales[rows, first : first + N],
                start=True,
                stop=True,
            )

        def combine(eng, op, dst, a, b):
            eng.tensor_tensor(out=dst, in0=a, in1=b, op=op)

        dy_runs = dy_rows.rearrange("p (i j) n -> p i (j n)", j=PAIR)
        for i in range(PACK // PAIR):
            load(dy_pair[i][:].rearrange("p j n -> p (j n)")[:, : N + EARLY], dy_runs[:, i, : N + EARLY])
        load(w_raw[:], w_rows)
        load(dy_late[:], dy_runs[:, :, N + EARLY :])
        load(mk_first[:], mk_rows[0])
        load(gs_first[:], gs_rows[0][:, 0, :])
        load(mk_third[:], mk_rows[1][:, 0, :])
        load(gs_second, gs_rows[0][:, 1, :])
        load(gs_late[:, 0, :], gs_rows[1][:, 0, :])
        load(mk_last[:], mk_rows[1][:, 1, :])
        load(gs_late[:, 1, :], gs_rows[1][:, 1, :])

        first_rows, other_rows, all_rows = slice(0, PAIR), slice(PAIR, PACK), slice(0, PACK)
        vec, act = nc.vector.tensor_copy, nc.scalar.copy
        quarter = P // 2
        interleave(vec, DY_AT, dy_pair[0][:, :, :VEC_EARLY], first_rows)
        interleave(act, DY_AT + VEC_EARLY, dy_pair[0][:, :, VEC_EARLY:EARLY], first_rows)
        interleave(act, DY_AT + EARLY, dy_pair[0][:, :1, EARLY:], slice(0, 1))
        for lo, hi in ((0, P), (P, VEC_EARLY)):
            interleave(vec, DY_AT + lo, dy_pair[1][:, :, lo:hi], other_rows)
        interleave(act, DY_AT + VEC_EARLY, dy_pair[1][:, :, VEC_EARLY:EARLY], other_rows)
        interleave(act, DY_AT + EARLY, dy_pair[1][:, :1, EARLY:], slice(PAIR, PAIR + 1))
        for lo in range(DY_AT, DY_AT + EARLY, P):
            quantize(lo, lo + P)

        interleave(act, W_AT[0] + VEC_W, w_raw[:, :, VEC_W:P], all_rows)
        interleave(act, W_AT[1] + VEC_W_SECOND, w_raw[:, :, P + VEC_W_SECOND :], all_rows)
        interleave(act, DY_AT + EARLY, dy_late[:], slice(1, PACK, PAIR))
        interleave(vec, W_AT[0], w_raw[:, :, :quarter], all_rows)
        interleave(vec, W_AT[0] + quarter, w_raw[:, :, quarter:VEC_W], all_rows)
        for lo in (0, quarter):
            quantize(W_AT[0] + lo, W_AT[0] + lo + quarter)
        for g in range(G):
            multiply(z_early[g], 0, g, W_AT[0])
        interleave(vec, W_AT[1], w_raw[:, :, P : P + VEC_W_SECOND], all_rows)
        quantize(DY_AT + EARLY, DY_AT + N)
        quantize(W_AT[1], W_AT[1] + P)
        for h in range(HALVES):
            for g in range(G):
                multiply(z[h][g], h, g, DY_AT)

        combine(nc.vector, MULT, masked[0][:, 0, :EARLY], z_early[0][:, N - EARLY :], mk_first[:, 0, :EARLY])
        combine(nc.gpsimd, ADD, res_first[:, 0, :POOL_COLS], masked[0][:, 0, :POOL_COLS], gs_first[:, :POOL_COLS])
        combine(nc.vector, MULT, masked[0][:, 1, :EARLY], z_early[1][:, N - EARLY :], mk_first[:, 1, :EARLY])
        for g in range(G):
            combine(nc.vector, MULT, masked[0][:, g, EARLY:], z[0][g][:, EARLY:], mk_first[:, g, EARLY:])
        combine(nc.vector, MULT, masked[1][:, 0, :], z[1][0][:], mk_third[:])
        combine(nc.vector, ADD, res_first[:, 0, POOL_COLS:], masked[0][:, 0, POOL_COLS:], gs_first[:, POOL_COLS:])
        nc.sync.dma_start(out=out_rows[0][:, 0, :], in_=res_first[:, 0, :])
        combine(nc.vector, ADD, res_first[:, 1, :], masked[0][:, 1, :], gs_second)
        nc.sync.dma_start(out=out_rows[0][:, 1, :], in_=res_first[:, 1, :])
        for eng, lo, hi in ((nc.vector, 0, N - POOL_LATE), (nc.gpsimd, N - POOL_LATE, N)):
            combine(eng, ADD, res_third[:, lo:hi], masked[1][:, 0, lo:hi], gs_late[:, 0, lo:hi])
        nc.sync.dma_start(out=out_rows[1][:, 0, :], in_=res_third)
        half = N // 2
        for lo in (0, half):
            combine(nc.vector, MULT, masked[1][:, 1, lo : lo + half], z[1][1][:, lo : lo + half], mk_last[:, lo : lo + half])
        combine(nc.vector, ADD, res_last[:, :half], masked[1][:, 1, :half], gs_late[:, 1, :half])
        nc.sync.dma_start(out=out_rows[1][:, 1, :half], in_=res_last[:, :half])
        combine(nc.vector, ADD, res_last[:, half:], masked[1][:, 1, half:], gs_late[:, 1, half:])
        nc.sync.dma_start(out=out_rows[1][:, 1, half:], in_=res_last[:, half:])
